import numpy as np
import ml_dtypes


def mxq(x, axis, fmt="e4m3"):
    dtype, down = {"e4m3": (ml_dtypes.float8_e4m3fn, 7), "e5m2": (ml_dtypes.float8_e5m2, 14)}[fmt]
    v = np.moveaxis(np.asarray(x, np.float32).astype(ml_dtypes.bfloat16).astype(np.float64), axis, -1)
    blocks = v.reshape(v.shape[:-1] + (-1, 32))
    amax = np.abs(blocks).max(-1, keepdims=True)
    byte = np.maximum(np.where(amax > 0, np.frexp(amax)[1] - 1 + 127, 0) - down, 1)
    scale = np.exp2(byte - 127.0)
    codes = (blocks / scale).astype(np.float32).astype(dtype).astype(np.float64)
    return np.moveaxis((codes * scale).reshape(v.shape), -1, axis)


WIDE = False


def mx_kscale(k):
    if not WIDE:
        return np.ones(k)
    levels = np.array([18, -18])
    if k % 512:
        return np.exp2(np.random.permutation(np.resize(levels, k // 32))).repeat(32)
    a = np.empty((k // 512, 16))
    for p in range(k // 512):
        a[p, :8] = np.random.permutation(np.resize(levels, 8))
        for g in range(8):
            far = levels[np.abs(levels - a[p, g]) >= 10]
            a[p, g + 8] = far[np.random.randint(len(far))]
    return np.exp2(a.ravel()).repeat(32)


def f64(x):
    return np.asarray(x).astype(np.float64)


def striped(idx):
    return np.tile(np.asarray(idx).reshape(-1, 16).T, (8, 1)).astype(np.uint16)


def unstriped(offs):
    return offs[:16].T.reshape(-1).astype(np.int64)

def planes(y):
    n, m = y.shape
    v = y.astype(np.float32).astype(ml_dtypes.bfloat16).astype(np.float64).reshape(n // 32, 32, m)
    top = np.abs(v).max(1)
    byte = np.clip(np.where(top > 0, np.frexp(top)[1] - 1 + 127 - 7, 1), 1, 254)
    codes = (v * np.exp2(127.0 - byte)[:, None, :]).reshape(n, m).astype(np.float32).astype(ml_dtypes.float8_e4m3fn).view(np.uint8)
    words = codes.reshape(n // 512, 128, 4, m).transpose(0, 1, 3, 2)
    return np.ascontiguousarray(words), np.ascontiguousarray(byte.astype(np.uint8).reshape(n // 512, 16, m))


B, N, T, D, R = 1, 512, 2048, 512, 512


def setup_inputs():
    n = np.random.standard_normal
    idx = np.random.permutation(T)[:B * N]
    s = mx_kscale(D)[:, None]
    u = np.ones(T)
    u[idx] = mx_kscale(B * N)
    r = np.random.uniform(0.5, 2.0, T) * u
    x = n((B, D, R))
    return {
        "xT": (x * s).astype(np.float32),
        "wT": (n((D, T)) * (1.00 / np.sqrt(D)) / s / r).astype(np.float32),
        "y": n((B, R, N)).astype(np.float32),
        "wt": (np.random.uniform(0.5, 1.5, (B, R, 1)) * 1.0 / np.sqrt(R)).astype(np.float32),
        "ts": np.tile(r, (128, 1)).astype(np.float32),
        "offs": striped(idx),
    }


def reference(xT, wT, y, wt, ts, offs):
    idx = unstriped(offs)
    pick = lambda x: x[:, idx].reshape(x.shape[0], B, N).transpose(1, 0, 2)
    w = pick(f64(wT))
    a = mxq(f64(xT), 1, "e4m3").transpose(0, 2, 1) @ mxq(w, 1, "e4m3")
    ts_ = pick(f64(ts))[:, :1, :]
    a = a * ts_
    g = f64(wt) * np.tanh(a - f64(y))
    g = g * ts_
    gx = mxq(g, 2, "e5m2") @ mxq(w, 2, "e4m3").transpose(0, 2, 1)
    out_0 = gx
    return (out_0,) + planes(out_0[0])

@@ -1,0 +1,243 @@
+from contextlib import ExitStack
+
+import concourse.mybir as mybir
+from concourse.masks import make_identity
+
+N, T, D, R = 512, 2048, 512, 512
+FLOPS = 2 * 2 * N * D * R
+BYTES = 4 * (D * R + D * T + R * N + R + T + R * D) + 2 * 128 * (N // 16) + R * D + (R // 32) * D
+
+F32 = mybir.dt.float32
+BF16 = mybir.dt.bfloat16
+I32 = mybir.dt.int32
+U32 = mybir.dt.uint32
+U16 = mybir.dt.uint16
+U8 = mybir.dt.uint8
+E4M3 = mybir.dt.float8_e4m3fn_x4
+E5M2 = mybir.dt.float8_e5m2_x4
+MULT = mybir.AluOpType.mult
+SUB = mybir.AluOpType.subtract
+COPY = mybir.ActivationFunctionType.Copy
+TANH = mybir.ActivationFunctionType.Tanh
+
+P = 128
+L = 4
+
+
+def tile_attend_glch_pl_x_ts_kernel(tc, xT, wT, y, wt, ts, offs, out_0, out_1, out_2):
+    nc = tc.nc
+    lanes = range(L)
+    with ExitStack() as ctx:
+        sb = ctx.enter_context(tc.tile_pool(name="sb", bufs=1))
+        ps = ctx.enter_context(tc.psum_pool(name="ps", bufs=1))
+
+        def sbuf(name, shape, dtype, tag=None):
+            return sb.tile(shape, dtype, name=name, tag=tag or name, align_bytes=64)
+
+        offsets = sb.tile([P, N // 16], U16, name="offsets")
+        nc.sync.dma_start(offsets[:], offs)
+
+        ts_win = sbuf("ts_win", [P, T], F32)
+        nc.vector.memset(ts_win[:, : T // 2], 0.0)
+        nc.gpsimd.memset(ts_win[:, T // 2 :], 0.0)
+        warm = sbuf("warm", [P, 8], F32)
+        nc.vector.memset(warm[:], 0.0)
+        warm_out = sbuf("warm_out", [P, 8], F32)
+        nc.scalar.activation(warm_out[:], warm[:], TANH)
+
+        wt_col = sbuf("wt_col", [P, L], F32)
+        nc.sync.dma_start(wt_col[:], wt[0].rearrange("(m t) o -> m (t o)", t=L))
+        x_raw = sbuf("x_raw", [P, L, R], F32)
+        nc.sync.dma_start(x_raw[:], xT[0].rearrange("(p j) r -> p j r", j=L))
+        nc.sync.dma_start(ts_win[0:1, :], ts[0:1, :])
+        w_rows = wT.rearrange("(p j) c -> p j c", j=L)
+        y_rows = y[0].rearrange("(m t) i -> m t i", t=L)
+        w_win = [sbuf("w_win%d" % j, [P, T], F32) for j in lanes]
+        y_raw = [sbuf("y_raw%d" % t, [P, N], F32) for t in lanes]
+        nc.sync.dma_start(w_win[0][:], w_rows[:, 0, :])
+        for j in range(1, L):
+            nc.sync.dma_start(w_win[j][:], w_rows[:, j, :])
+            nc.sync.dma_start(y_raw[j - 1][:], y_rows[:, j - 1, :])
+        nc.sync.dma_start(y_raw[L - 1][:], y_rows[:, L - 1, :])
+
+        ident_f = sbuf("ident_f", [P, P], F32)
+        make_identity(nc, ident_f[:])
+        ident_b = sbuf("ident_b", [P, P], BF16)
+        make_identity(nc, ident_b[:])
+
+        wt_ps = ps.tile([P, L, P], F32, name="wt_ps", tag="wt_ps")
+        for t in lanes:
+            nc.tensor.transpose(wt_ps[:, t, :], wt_col[:, t : t + 1].to_broadcast([P, P]), ident_f[:])
+
+        x_b = sbuf("x_b", [P, L, P, L], BF16)
+        nc.vector.tensor_copy(
+            x_b[:].rearrange("p t m j -> p m j t"),
+            x_raw[:].rearrange("p j (m t) -> p m j t", t=L),
+        )
+        ts_g = sbuf("ts_g", [P, N], F32)
+        nc.vector.tensor_copy(ts_g[:], ts_win[:].indirect(offsets[:]))
+        x_q = sbuf("x_q", [P, R], U32)
+        x_s = sbuf("x_s", [P, R], U8)
+        nc.vector.quantize_mx(x_q[:].bitcast(E4M3), x_s[:], x_b[:].rearrange("p t m j -> p (t m j)"))
+
+        ts_ps = ps.tile([P, L, P], F32, name="ts_ps", tag="turn_a")
+        for s in lanes:
+            nc.tensor.transpose(ts_ps[:, s, :], ts_g[:, s::L], ident_f[:])
+        ts_col = sbuf("ts_col", [P, L], F32)
+        nc.scalar.copy(ts_col[:], ts_ps[:, :, 0])
+        factor = sbuf("factor", [P, L, L, P], F32)
+        for s in lanes:
+            nc.scalar.activation(factor[:, s, :, :], wt_ps[:], COPY, scale=ts_col[:, s : s + 1])
+
+        w_b = sbuf("w_b", [P, L, P, L], BF16)
+        w_flat = sbuf("w_flat", [P, (L - 1) * N], BF16)
+        v_b = sbuf("v_b", [P, L * N], BF16)
+        y_t = [sbuf("y_t%d" % t, [P, L, P], F32) for t in lanes]
+
+        def gather(j):
+            nc.vector.tensor_copy(w_flat[:, j * N : (j + 1) * N], w_win[j][:].indirect(offsets[:]))
+
+        def turn_w(j, bank):
+            w_ps = ps.tile([P, 2, P], F32, name="w_ps%d" % j, tag=bank)
+            words = w_flat[:, j * N : (j + 1) * N].bitcast(F32)
+            for u in range(2):
+                nc.tensor.transpose(w_ps[:, u, :], words[:, u::2], ident_f[:])
+            nc.scalar.copy(
+                v_b[:, j * N : (j + 1) * N].bitcast(F32).rearrange("m (p u) -> m p u", u=2),
+                w_ps[:].rearrange("m u p -> m p u"),
+            )
+
+        def turn_y(t, bank):
+            y_ps = ps.tile([P, L, P], F32, name="y_ps%d" % t, tag=bank)
+            for s in lanes:
+                nc.tensor.transpose(y_ps[:, s, :], y_raw[t][:, s::L], ident_f[:])
+            nc.scalar.copy(y_t[t][:], y_ps[:])
+
+        gather(0)
+        turn_w(0, "turn_b")
+        gather(1)
+        turn_w(1, "turn_a")
+        turn_y(0, "turn_b")
+        gather(2)
+        turn_w(2, "turn_a")
+        turn_y(1, "turn_b")
+        nc.vector.tensor_copy(
+            w_b[:, :, :, 0 : L - 1].rearrange("p s m j -> p m j s"),
+            w_flat[:].rearrange("p (j m s) -> p m j s", j=L - 1, s=L),
+        )
+        turn_y(2, "turn_a")
+        nc.vector.tensor_copy(w_b[:, :, :, L - 1].rearrange("p s m -> p m s"), w_win[L - 1][:].indirect(offsets[:]))
+        w_q = sbuf("w_q", [P, N], U32)
+        w_s = sbuf("w_s", [P, N], U8)
+        nc.vector.quantize_mx(w_q[:].bitcast(E4M3), w_s[:], w_b[:].rearrange("p s m j -> p (s m j)"))
+
+        w_ps = ps.tile([P, L, P], BF16, name="w_ps3", tag="turn_c")
+        for s in lanes:
+            nc.tensor.transpose(w_ps[:, s, :], w_b[:, s, :, L - 1], ident_b[:])
+        nc.scalar.copy(
+            v_b[:, (L - 1) * N :].rearrange("m (p s) -> m p s", s=L), w_ps[:].rearrange("m s p -> m p s")
+        )
+        v_q = sbuf("v_q", [P, D], U32, tag="w_win3")
+        v_s = sbuf("v_s", [P, D], U8)
+
+        def quant_v(first, last):
+            cols = slice(first * P, last * P)
+            nc.vector.quantize_mx(v_q[:, cols].bitcast(E4M3), v_s[:, cols], v_b[:, first * N : last * N])
+
+        quant_v(0, 2)
+        quant_v(2, 3)
+
+        score = []
+        for t in lanes:
+            bank = ps.tile([P, L, P], F32, name="score%d" % t, tag="mx%d" % t)
+            score.append(bank)
+            rows = slice(t * P, (t + 1) * P)
+            for s in lanes:
+                slots = slice(s * P, (s + 1) * P)
+                nc.tensor.matmul_mx(
+                    bank[:, s, :],
+                    lhsT=w_q[:, slots].bitcast(E4M3),
+                    lhsT_scale=w_s[:, slots],
+                    rhs=x_q[:, rows].bitcast(E4M3),
+                    rhs_scale=x_s[:, rows],
+                    start=True,
+                    stop=True,
+                )
+            if t == 1:
+                turn_y(3, "turn_c")
+
+        z = [sbuf("z%d" % t, [P, L, P], F32) for t in lanes]
+        th = [sbuf("th%d" % t, [P, L, P], F32) for t in lanes]
+        h_b = [sbuf("h_b%d" % t, [P, P, L], BF16) for t in lanes]
+        h_q = [sbuf("h_q%d" % t, [P, P], U32) for t in lanes]
+        h_s = [sbuf("h_s%d" % t, [P, P], U8) for t in lanes]
+        g = sbuf("g", [P, L * D], F32)
+        out_rows = out_0[0].rearrange("(m t) d -> m t d", t=L)
+
+        def residual(t):
+            for s in lanes:
+                nc.vector.scalar_tensor_tensor(
+                    z[t][:, s, :], score[t][:, s, :], ts_col[:, s : s + 1], y_t[t][:, s, :], MULT, SUB
+                )
+            nc.scalar.activation(th[t][:], z[t][:], TANH)
+
+        def weigh(t):
+            nc.vector.tensor_tensor(
+                h_b[t][:].rearrange("p (c i) s -> p c s i", i=L),
+                th[t][:].rearrange("p s (c i) -> p c s i", i=L),
+                factor[:, :, t, :].rearrange("p s (c i) -> p c s i", i=L),
+                MULT,
+            )
+
+        def back(t, parts):
+            nc.vector.quantize_mx(h_q[t][:].bitcast(E5M2), h_s[t][:], h_b[t][:].rearrange("p m s -> p (m s)"))
+            acc = ps.tile([P, L, P], F32, name="acc%d" % t, tag="mx%d" % t)
+            nc.tensor.matmul_mx(
+                acc[:].rearrange("m j p -> m (j p)"),
+                lhsT=h_q[t][:].bitcast(E5M2),
+                lhsT_scale=h_s[t][:],
+                rhs=v_q[:].bitcast(E4M3),
+                rhs_scale=v_s[:],
+                start=True,
+                stop=True,
+            )
+            width = D // parts
+            for k in range(parts):
+                nc.scalar.copy(
+                    g[:, t * D + k * width : t * D + (k + 1) * width].rearrange("m (p j) -> m p j", j=L),
+                    acc[:, :, k * width // L : (k + 1) * width // L].rearrange("m j p -> m p j"),
+                )
+            nc.sync.dma_start(out_rows[:, t, :], g[:, t * D : (t + 1) * D])
+
+        for step in range(L + 2):
+            if step < L:
+                residual(step)
+            if step == 1:
+                quant_v(3, 4)
+            if step >= 2:
+                back(step - 2, 2 if step == L + 1 else 1)
+            if 1 <= step <= L:
+                weigh(step - 1)
+
+        g_b = sbuf("g_b", [P, D, L], BF16)
+        g_q = sbuf("g_q", [P, D], U32)
+        g_s = sbuf("g_s", [P, D], U8)
+        nc.vector.tensor_copy(
+            g_b[:, :, 0 : L - 1].rearrange("p (c i) t -> p c t i", i=L),
+            g[:, 0 : (L - 1) * D].rearrange("p (t c i) -> p c t i", t=L - 1, i=L),
+        )
+        half = D // 2
+        words_out = out_1[0].rearrange("p d l -> p (d l)").bitcast(I32)
+        for k in range(2):
+            cols = slice(k * half, (k + 1) * half)
+            nc.vector.tensor_copy(g_b[:, cols, L - 1], g[:, (L - 1) * D + k * half : (L - 1) * D + (k + 1) * half])
+        for k in range(2):
+            cols = slice(k * half, (k + 1) * half)
+            nc.vector.quantize_mx(
+                g_q[:, cols].bitcast(E4M3), g_s[:, cols], g_b[:, cols, :].rearrange("p d t -> p (d t)")
+            )
+            nc.sync.dma_start(words_out[:, cols], g_q[:, cols].bitcast(I32))
+        scale_rows = out_2[0].bitcast(I32)
+        for q in lanes:
+            eng = nc.scalar if q % 2 == 0 else nc.sync
+            eng.dma_start(scale_rows[L * q : L * (q + 1), :], g_s[32 * q : 32 * q + L, :].bitcast(I32))

@@ -17,7 +17,6 @@ E4M3 = mybir.dt.float8_e4m3fn_x4
 E5M2 = mybir.dt.float8_e5m2_x4
 MULT = mybir.AluOpType.mult
 SUB = mybir.AluOpType.subtract
-COPY = mybir.ActivationFunctionType.Copy
 TANH = mybir.ActivationFunctionType.Tanh
 
 P = 128
@@ -53,12 +52,14 @@ def tile_attend_glch_pl_x_ts_kernel(tc, xT, wT, y, wt, ts, offs, out_0, out_1, o
         w_rows = wT.rearrange("(p j) c -> p j c", j=L)
         y_rows = y[0].rearrange("(m t) i -> m t i", t=L)
         w_win = [sbuf("w_win%d" % j, [P, T], F32) for j in lanes]
-        y_raw = [sbuf("y_raw%d" % t, [P, N], F32) for t in lanes]
-        nc.sync.dma_start(w_win[0][:], w_rows[:, 0, :])
-        for j in range(1, L):
+        y_early = sbuf("y_early", [P, 2, N], F32)
+        y_late = [sbuf("y_late%d" % k, [P, N], F32) for k in range(2)]
+        for j in lanes:
             nc.sync.dma_start(w_win[j][:], w_rows[:, j, :])
-            nc.sync.dma_start(y_raw[j - 1][:], y_rows[:, j - 1, :])
-        nc.sync.dma_start(y_raw[L - 1][:], y_rows[:, L - 1, :])
+            if j == 1:
+                nc.sync.dma_start(y_early[:], y_rows[:, 0:2, :])
+            if j >= 2:
+                nc.sync.dma_start(y_late[j - 2][:], y_rows[:, j, :])
 
         ident_f = sbuf("ident_f", [P, P], F32)
         make_identity(nc, ident_f[:])
@@ -70,10 +71,10 @@ def tile_attend_glch_pl_x_ts_kernel(tc, xT, wT, y, wt, ts, offs, out_0, out_1, o
             nc.tensor.transpose(wt_ps[:, t, :], wt_col[:, t : t + 1].to_broadcast([P, P]), ident_f[:])
 
         x_b = sbuf("x_b", [P, L, P, L], BF16)
-        nc.vector.tensor_copy(
-            x_b[:].rearrange("p t m j -> p m j t"),
-            x_raw[:].rearrange("p j (m t) -> p m j t", t=L),
-        )
+        x_to = x_b[:].rearrange("p t m j -> p m j t")
+        x_from = x_raw[:].rearrange("p j (m t) -> p m j t", t=L)
+        nc.vector.tensor_copy(x_to[:, : P // 2], x_from[:, : P // 2])
+        nc.scalar.copy(x_to[:, P // 2 :], x_from[:, P // 2 :])
         ts_g = sbuf("ts_g", [P, N], F32)
         nc.vector.tensor_copy(ts_g[:], ts_win[:].indirect(offsets[:]))
         x_q = sbuf("x_q", [P, R], U32)
@@ -85,14 +86,20 @@ def tile_attend_glch_pl_x_ts_kernel(tc, xT, wT, y, wt, ts, offs, out_0, out_1, o
             nc.tensor.transpose(ts_ps[:, s, :], ts_g[:, s::L], ident_f[:])
         ts_col = sbuf("ts_col", [P, L], F32)
         nc.scalar.copy(ts_col[:], ts_ps[:, :, 0])
-        factor = sbuf("factor", [P, L, L, P], F32)
-        for s in lanes:
-            nc.scalar.activation(factor[:, s, :, :], wt_ps[:], COPY, scale=ts_col[:, s : s + 1])
+        factor = [sbuf("factor%d" % t, [P, P, L], F32) for t in lanes]
+
+        def make_factor(t):
+            nc.vector.tensor_tensor(
+                factor[t][:],
+                wt_ps[:, t, :].unsqueeze(2).broadcast_to([P, P, L]),
+                ts_col[:].unsqueeze(1).broadcast_to([P, P, L]),
+                MULT,
+            )
 
         w_b = sbuf("w_b", [P, L, P, L], BF16)
         w_flat = sbuf("w_flat", [P, (L - 1) * N], BF16)
         v_b = sbuf("v_b", [P, L * N], BF16)
-        y_t = [sbuf("y_t%d" % t, [P, L, P], F32) for t in lanes]
+        y_t = [sbuf("y_t%d" % u, [P, L, 2, P], F32) for u in range(2)]
 
         def gather(j):
             nc.vector.tensor_copy(w_flat[:, j * N : (j + 1) * N], w_win[j][:].indirect(offsets[:]))
@@ -107,29 +114,40 @@ def tile_attend_glch_pl_x_ts_kernel(tc, xT, wT, y, wt, ts, offs, out_0, out_1, o
                 w_ps[:].rearrange("m u p -> m p u"),
             )
 
-        def turn_y(t, bank):
+        def turn_y(t, bank, slot_lanes):
             y_ps = ps.tile([P, L, P], F32, name="y_ps%d" % t, tag=bank)
             for s in lanes:
-                nc.tensor.transpose(y_ps[:, s, :], y_raw[t][:, s::L], ident_f[:])
-            nc.scalar.copy(y_t[t][:], y_ps[:])
+                nc.tensor.transpose(y_ps[:, s, :], slot_lanes[s], ident_f[:])
+            nc.scalar.copy(y_t[t // 2][:, :, t % 2, :], y_ps[:])
 
         gather(0)
         turn_w(0, "turn_b")
+        make_factor(0)
+        make_factor(1)
         gather(1)
         turn_w(1, "turn_a")
-        turn_y(0, "turn_b")
+        make_factor(2)
+        make_factor(3)
+        turn_y(0, "turn_b", [y_early[:, 0, s::L] for s in lanes])
+        turn_y(1, "turn_a", [y_early[:, 1, s::L] for s in lanes])
         gather(2)
-        turn_w(2, "turn_a")
-        turn_y(1, "turn_b")
+        turn_w(2, "turn_b")
         nc.vector.tensor_copy(
             w_b[:, :, :, 0 : L - 1].rearrange("p s m j -> p m j s"),
             w_flat[:].rearrange("p (j m s) -> p m j s", j=L - 1, s=L),
         )
-        turn_y(2, "turn_a")
+        turn_y(2, "turn_a", [y_late[0][:, s::L] for s in lanes])
+        turn_y(3, "turn_b", [y_late[1][:, s::L] for s in lanes])
         nc.vector.tensor_copy(w_b[:, :, :, L - 1].rearrange("p s m -> p m s"), w_win[L - 1][:].indirect(offsets[:]))
         w_q = sbuf("w_q", [P, N], U32)
         w_s = sbuf("w_s", [P, N], U8)
-        nc.vector.quantize_mx(w_q[:].bitcast(E4M3), w_s[:], w_b[:].rearrange("p s m j -> p (s m j)"))
+        for k in range(2):
+            slots = slice(k * N // 2, (k + 1) * N // 2)
+            nc.vector.quantize_mx(
+                w_q[:, slots].bitcast(E4M3),
+                w_s[:, slots],
+                w_b[:, 2 * k : 2 * k + 2].rearrange("p s m j -> p (s m j)"),
+            )
 
         w_ps = ps.tile([P, L, P], BF16, name="w_ps3", tag="turn_c")
         for s in lanes:
@@ -137,6 +155,7 @@ def tile_attend_glch_pl_x_ts_kernel(tc, xT, wT, y, wt, ts, offs, out_0, out_1, o
         nc.scalar.copy(
             v_b[:, (L - 1) * N :].rearrange("m (p s) -> m p s", s=L), w_ps[:].rearrange("m s p -> m p s")
         )
+
         v_q = sbuf("v_q", [P, D], U32, tag="w_win3")
         v_s = sbuf("v_s", [P, D], U8)
 
@@ -148,46 +167,50 @@ def tile_attend_glch_pl_x_ts_kernel(tc, xT, wT, y, wt, ts, offs, out_0, out_1, o
         quant_v(2, 3)
 
         score = []
-        for t in lanes:
-            bank = ps.tile([P, L, P], F32, name="score%d" % t, tag="mx%d" % t)
-            score.append(bank)
-            rows = slice(t * P, (t + 1) * P)
-            for s in lanes:
-                slots = slice(s * P, (s + 1) * P)
-                nc.tensor.matmul_mx(
-                    bank[:, s, :],
-                    lhsT=w_q[:, slots].bitcast(E4M3),
-                    lhsT_scale=w_s[:, slots],
-                    rhs=x_q[:, rows].bitcast(E4M3),
-                    rhs_scale=x_s[:, rows],
-                    start=True,
-                    stop=True,
-                )
-            if t == 1:
-                turn_y(3, "turn_c")
+        for u in range(2):
+            rows = slice(u * 2 * P, (u + 1) * 2 * P)
+            for v in range(2):
+                bank = ps.tile([P, 2, 2 * P], F32, name="score%d%d" % (u, v), tag="mx%d" % (2 * u + v))
+                score.append(bank)
+                for e in range(2):
+                    slots = slice((2 * v + e) * P, (2 * v + e + 1) * P)
+                    nc.tensor.matmul_mx(
+                        bank[:, e, :],
+                        lhsT=w_q[:, slots].bitcast(E4M3),
+                        lhsT_scale=w_s[:, slots],
+                        rhs=x_q[:, rows].bitcast(E4M3),
+                        rhs_scale=x_s[:, rows],
+                        start=True,
+                        stop=True,
+                    )
 
-        z = [sbuf("z%d" % t, [P, L, P], F32) for t in lanes]
-        th = [sbuf("th%d" % t, [P, L, P], F32) for t in lanes]
+        z = [sbuf("z%d" % u, [P, L, 2, P], F32) for u in range(2)]
+        th = [sbuf("th%d" % t, [P, P, L], F32) for t in lanes]
         h_b = [sbuf("h_b%d" % t, [P, P, L], BF16) for t in lanes]
         h_q = [sbuf("h_q%d" % t, [P, P], U32) for t in lanes]
         h_s = [sbuf("h_s%d" % t, [P, P], U8) for t in lanes]
         g = sbuf("g", [P, L * D], F32)
         out_rows = out_0[0].rearrange("(m t) d -> m t d", t=L)
 
-        def residual(t):
+        def residual(u):
             for s in lanes:
                 nc.vector.scalar_tensor_tensor(
-                    z[t][:, s, :], score[t][:, s, :], ts_col[:, s : s + 1], y_t[t][:, s, :], MULT, SUB
+                    z[u][:, s].rearrange("p e m -> p (e m)"),
+                    score[2 * u + s // 2][:, s % 2, :],
+                    ts_col[:, s : s + 1],
+                    y_t[u][:, s].rearrange("p e m -> p (e m)"),
+                    MULT,
+                    SUB,
                 )
-            nc.scalar.activation(th[t][:], z[t][:], TANH)
+            for e in range(2):
+                nc.scalar.activation(
+                    th[2 * u + e][:].rearrange("p (c i) s -> p c s i", i=L),
+                    z[u][:, :, e, :].rearrange("p s (c i) -> p c s i", i=L),
+                    TANH,
+                )
 
         def weigh(t):
-            nc.vector.tensor_tensor(
-                h_b[t][:].rearrange("p (c i) s -> p c s i", i=L),
-                th[t][:].rearrange("p s (c i) -> p c s i", i=L),
-                factor[:, :, t, :].rearrange("p s (c i) -> p c s i", i=L),
-                MULT,
-            )
+            nc.vector.tensor_tensor(h_b[t][:], th[t][:], factor[t][:], MULT)
 
         def back(t, parts):
             nc.vector.quantize_mx(h_q[t][:].bitcast(E5M2), h_s[t][:], h_b[t][:].rearrange("p m s -> p (m s)"))
@@ -209,28 +232,28 @@ def tile_attend_glch_pl_x_ts_kernel(tc, xT, wT, y, wt, ts, offs, out_0, out_1, o
                 )
             nc.sync.dma_start(out_rows[:, t, :], g[:, t * D : (t + 1) * D])
 
-        for step in range(L + 2):
-            if step < L:
-                residual(step)
-            if step == 1:
-                quant_v(3, 4)
-            if step >= 2:
-                back(step - 2, 2 if step == L + 1 else 1)
-            if 1 <= step <= L:
-                weigh(step - 1)
+        residual(0)
+        quant_v(3, 4)
+        residual(1)
+        weigh(0)
+        for t in range(1, L - 1):
+            weigh(t)
+            back(t - 1, 1)
+        back(L - 2, 1)
+        weigh(L - 1)
+        back(L - 1, 2)
 
         g_b = sbuf("g_b", [P, D, L], BF16)
         g_q = sbuf("g_q", [P, D], U32)
         g_s = sbuf("g_s", [P, D], U8)
-        nc.vector.tensor_copy(
-            g_b[:, :, 0 : L - 1].rearrange("p (c i) t -> p c t i", i=L),
-            g[:, 0 : (L - 1) * D].rearrange("p (t c i) -> p c t i", t=L - 1, i=L),
-        )
+        g_from = g[:].rearrange("p (t c i) -> p c t i", t=L, i=L)
+        g_to = g_b[:].rearrange("p (c i) t -> p c t i", i=L)
+        nc.vector.tensor_copy(g_to[:, :, 0:2], g_from[:, :, 0:2])
         half = D // 2
         words_out = out_1[0].rearrange("p d l -> p (d l)").bitcast(I32)
         for k in range(2):
-            cols = slice(k * half, (k + 1) * half)
-            nc.vector.tensor_copy(g_b[:, cols, L - 1], g[:, (L - 1) * D + k * half : (L - 1) * D + (k + 1) * half])
+            runs = slice(k * half // L, (k + 1) * half // L)
+            nc.vector.tensor_copy(g_to[:, runs, 2:L], g_from[:, runs, 2:L])
         for k in range(2):
             cols = slice(k * half, (k + 1) * half)
             nc.vector.quantize_mx(

@@ -34,7 +34,6 @@ def tile_attend_glch_pl_x_ts_kernel(tc, xT, wT, y, wt, ts, offs, out_0, out_1, o
             return sb.tile(shape, dtype, name=name, tag=tag or name, align_bytes=64)
 
         offsets = sb.tile([P, N // 16], U16, name="offsets")
-        nc.sync.dma_start(offsets[:], offs)
 
         ts_win = sbuf("ts_win", [P, T], F32)
         nc.vector.memset(ts_win[:, : T // 2], 0.0)
@@ -44,10 +43,11 @@ def tile_attend_glch_pl_x_ts_kernel(tc, xT, wT, y, wt, ts, offs, out_0, out_1, o
         warm_out = sbuf("warm_out", [P, 8], F32)
         nc.scalar.activation(warm_out[:], warm[:], TANH)
 
-        wt_col = sbuf("wt_col", [P, L], F32)
-        nc.sync.dma_start(wt_col[:], wt[0].rearrange("(m t) o -> m (t o)", t=L))
         x_raw = sbuf("x_raw", [P, L, R], F32)
         nc.sync.dma_start(x_raw[:], xT[0].rearrange("(p j) r -> p j r", j=L))
+        nc.sync.dma_start(offsets[:], offs)
+        wt_col = sbuf("wt_col", [P, L], F32)
+        nc.sync.dma_start(wt_col[:], wt[0].rearrange("(m t) o -> m (t o)", t=L))
         nc.sync.dma_start(ts_win[0:1, :], ts[0:1, :])
         w_rows = wT.rearrange("(p j) c -> p j c", j=L)
         y_rows = y[0].rearrange("(m t) i -> m t i", t=L)
@@ -186,7 +186,7 @@ def tile_attend_glch_pl_x_ts_kernel(tc, xT, wT, y, wt, ts, offs, out_0, out_1, o
 
         z = [sbuf("z%d" % u, [P, L, 2, P], F32) for u in range(2)]
         th = [sbuf("th%d" % t, [P, P, L], F32) for t in lanes]
-        h_b = [sbuf("h_b%d" % t, [P, P, L], BF16) for t in lanes]
+        h_b = []
         h_q = [sbuf("h_q%d" % t, [P, P], U32) for t in lanes]
         h_s = [sbuf("h_s%d" % t, [P, P], U8) for t in lanes]
         g = sbuf("g", [P, L * D], F32)
@@ -210,6 +210,7 @@ def tile_attend_glch_pl_x_ts_kernel(tc, xT, wT, y, wt, ts, offs, out_0, out_1, o
                 )
 
         def weigh(t):
+            h_b.append(sbuf("h_b%d" % t, [P, P, L], BF16, tag="h_b%d" % min(t, 2)))
             nc.vector.tensor_tensor(h_b[t][:], th[t][:], factor[t][:], MULT)
 
         def back(t, parts):

@@ -63,8 +63,6 @@ def tile_attend_glch_pl_x_ts_kernel(tc, xT, wT, y, wt, ts, offs, out_0, out_1, o
 
         ident_f = sbuf("ident_f", [P, P], F32)
         make_identity(nc, ident_f[:])
-        ident_b = sbuf("ident_b", [P, P], BF16)
-        make_identity(nc, ident_b[:])
 
         wt_ps = ps.tile([P, L, P], F32, name="wt_ps", tag="wt_ps")
         for t in lanes:
@@ -97,16 +95,18 @@ def tile_attend_glch_pl_x_ts_kernel(tc, xT, wT, y, wt, ts, offs, out_0, out_1, o
             )
 
         w_b = sbuf("w_b", [P, L, P, L], BF16)
-        w_flat = sbuf("w_flat", [P, (L - 1) * N], BF16)
+        w_early = sbuf("w_early", [P, (L - 1) * N], BF16)
+        w_last = sbuf("w_last", [P, N], BF16)
+        w_flat = [w_early[:, j * N : (j + 1) * N] for j in range(L - 1)] + [w_last[:]]
         v_b = sbuf("v_b", [P, L * N], BF16)
         y_t = [sbuf("y_t%d" % u, [P, L, 2, P], F32) for u in range(2)]
 
         def gather(j):
-            nc.vector.tensor_copy(w_flat[:, j * N : (j + 1) * N], w_win[j][:].indirect(offsets[:]))
+            nc.vector.tensor_copy(w_flat[j], w_win[j][:].indirect(offsets[:]))
 
         def turn_w(j, bank):
             w_ps = ps.tile([P, 2, P], F32, name="w_ps%d" % j, tag=bank)
-            words = w_flat[:, j * N : (j + 1) * N].bitcast(F32)
+            words = w_flat[j].bitcast(F32)
             for u in range(2):
                 nc.tensor.transpose(w_ps[:, u, :], words[:, u::2], ident_f[:])
             nc.scalar.copy(
@@ -132,61 +132,49 @@ def tile_attend_glch_pl_x_ts_kernel(tc, xT, wT, y, wt, ts, offs, out_0, out_1, o
         turn_y(1, "turn_a", [y_early[:, 1, s::L] for s in lanes])
         gather(2)
         turn_w(2, "turn_b")
-        nc.vector.tensor_copy(
-            w_b[:, :, :, 0 : L - 1].rearrange("p s m j -> p m j s"),
-            w_flat[:].rearrange("p (j m s) -> p m j s", j=L - 1, s=L),
-        )
+        w_to = w_b[:].rearrange("p s m j -> p m j s")
+        nc.vector.tensor_copy(w_to[:, :, 0 : L - 1], w_early[:].rearrange("p (j m s) -> p m j s", j=L - 1, s=L))
         turn_y(2, "turn_a", [y_late[0][:, s::L] for s in lanes])
         turn_y(3, "turn_b", [y_late[1][:, s::L] for s in lanes])
-        nc.vector.tensor_copy(w_b[:, :, :, L - 1].rearrange("p s m -> p m s"), w_win[L - 1][:].indirect(offsets[:]))
-        w_q = sbuf("w_q", [P, N], U32)
-        w_s = sbuf("w_s", [P, N], U8)
-        for k in range(2):
-            slots = slice(k * N // 2, (k + 1) * N // 2)
-            nc.vector.quantize_mx(
-                w_q[:, slots].bitcast(E4M3),
-                w_s[:, slots],
-                w_b[:, 2 * k : 2 * k + 2].rearrange("p s m j -> p (s m j)"),
-            )
-
-        w_ps = ps.tile([P, L, P], BF16, name="w_ps3", tag="turn_c")
-        for s in lanes:
-            nc.tensor.transpose(w_ps[:, s, :], w_b[:, s, :, L - 1], ident_b[:])
-        nc.scalar.copy(
-            v_b[:, (L - 1) * N :].rearrange("m (p s) -> m p s", s=L), w_ps[:].rearrange("m s p -> m p s")
-        )
-
+        gather(L - 1)
         v_q = sbuf("v_q", [P, D], U32, tag="w_win3")
         v_s = sbuf("v_s", [P, D], U8)
 
-        def quant_v(first, last):
-            cols = slice(first * P, last * P)
-            nc.vector.quantize_mx(v_q[:, cols].bitcast(E4M3), v_s[:, cols], v_b[:, first * N : last * N])
+        def quant_v(half):
+            cols = slice(half * D // 2, (half + 1) * D // 2)
+            nc.vector.quantize_mx(v_q[:, cols].bitcast(E4M3), v_s[:, cols], v_b[:, 2 * half * N : 2 * (half + 1) * N])
 
-        quant_v(0, 2)
-        quant_v(2, 3)
+        quant_v(0)
+        turn_w(L - 1, "turn_c")
+        w_q = sbuf("w_q", [P, N], U32)
+        w_s = sbuf("w_s", [P, N], U8)
+        last_from = w_last[:].rearrange("p (m s) -> p m s", s=L)
+        for v in range(2):
+            nc.vector.tensor_copy(w_to[:, :, L - 1, 2 * v : 2 * v + 2], last_from[:, :, 2 * v : 2 * v + 2])
+        for s in lanes:
+            slots = slice(s * P, (s + 1) * P)
+            nc.vector.quantize_mx(w_q[:, slots].bitcast(E4M3), w_s[:, slots], w_b[:, s].rearrange("p m j -> p (m j)"))
 
-        score = []
+        first = [ps.tile([P, 2 * P], F32, name="score0%d" % s, tag="mx%d" % s) for s in lanes]
+        second = [ps.tile([P, 2, 2 * P], F32, name="score1%d" % v, tag=("wt_ps", "turn_a")[v]) for v in range(2)]
+        score = [[first[s][:] for s in lanes], [second[s // 2][:, s % 2, :] for s in lanes]]
         for u in range(2):
             rows = slice(u * 2 * P, (u + 1) * 2 * P)
-            for v in range(2):
-                bank = ps.tile([P, 2, 2 * P], F32, name="score%d%d" % (u, v), tag="mx%d" % (2 * u + v))
-                score.append(bank)
-                for e in range(2):
-                    slots = slice((2 * v + e) * P, (2 * v + e + 1) * P)
-                    nc.tensor.matmul_mx(
-                        bank[:, e, :],
-                        lhsT=w_q[:, slots].bitcast(E4M3),
-                        lhsT_scale=w_s[:, slots],
-                        rhs=x_q[:, rows].bitcast(E4M3),
-                        rhs_scale=x_s[:, rows],
-                        start=True,
-                        stop=True,
-                    )
+            for s in lanes:
+                slots = slice(s * P, (s + 1) * P)
+                nc.tensor.matmul_mx(
+                    score[u][s],
+                    lhsT=w_q[:, slots].bitcast(E4M3),
+                    lhsT_scale=w_s[:, slots],
+                    rhs=x_q[:, rows].bitcast(E4M3),
+                    rhs_scale=x_s[:, rows],
+                    start=True,
+                    stop=True,
+                )
 
         z = [sbuf("z%d" % u, [P, L, 2, P], F32) for u in range(2)]
         th = [sbuf("th%d" % t, [P, P, L], F32) for t in lanes]
-        h_b = []
+        h_b = [sbuf("h_b%d" % t, [P, P * L], BF16) for t in lanes]
         h_q = [sbuf("h_q%d" % t, [P, P], U32) for t in lanes]
         h_s = [sbuf("h_s%d" % t, [P, P], U8) for t in lanes]
         g = sbuf("g", [P, L * D], F32)
@@ -196,7 +184,7 @@ def tile_attend_glch_pl_x_ts_kernel(tc, xT, wT, y, wt, ts, offs, out_0, out_1, o
             for s in lanes:
                 nc.vector.scalar_tensor_tensor(
                     z[u][:, s].rearrange("p e m -> p (e m)"),
-                    score[2 * u + s // 2][:, s % 2, :],
+                    score[u][s],
                     ts_col[:, s : s + 1],
                     y_t[u][:, s].rearrange("p e m -> p (e m)"),
                     MULT,
@@ -209,12 +197,21 @@ def tile_attend_glch_pl_x_ts_kernel(tc, xT, wT, y, wt, ts, offs, out_0, out_1, o
                     TANH,
                 )
 
-        def weigh(t):
-            h_b.append(sbuf("h_b%d" % t, [P, P, L], BF16, tag="h_b%d" % min(t, 2)))
-            nc.vector.tensor_tensor(h_b[t][:], th[t][:], factor[t][:], MULT)
+        def weigh(t, parts):
+            for k in range(parts):
+                rows = slice(k * P // parts, (k + 1) * P // parts)
+                nc.vector.tensor_tensor(
+                    h_b[t][:].rearrange("p (m s) -> p m s", s=L)[:, rows], th[t][:, rows], factor[t][:, rows], MULT
+                )
 
         def back(t, parts):
-            nc.vector.quantize_mx(h_q[t][:].bitcast(E5M2), h_s[t][:], h_b[t][:].rearrange("p m s -> p (m s)"))
+            for k in range(parts):
+                rows = slice(k * P // parts, (k + 1) * P // parts)
+                nc.vector.quantize_mx(
+                    h_q[t][:, rows].bitcast(E5M2),
+                    h_s[t][:, rows],
+                    h_b[t][:, k * P * L // parts : (k + 1) * P * L // parts],
+                )
             acc = ps.tile([P, L, P], F32, name="acc%d" % t, tag="mx%d" % t)
             nc.tensor.matmul_mx(
                 acc[:].rearrange("m j p -> m (j p)"),
@@ -234,15 +231,16 @@ def tile_attend_glch_pl_x_ts_kernel(tc, xT, wT, y, wt, ts, offs, out_0, out_1, o
             nc.sync.dma_start(out_rows[:, t, :], g[:, t * D : (t + 1) * D])
 
         residual(0)
-        quant_v(3, 4)
+        quant_v(1)
         residual(1)
-        weigh(0)
-        for t in range(1, L - 1):
-            weigh(t)
-            back(t - 1, 1)
-        back(L - 2, 1)
-        weigh(L - 1)
-        back(L - 1, 2)
+        weigh(0, 1)
+        weigh(1, 1)
+        back(0, 1)
+        weigh(2, 1)
+        back(1, 1)
+        back(2, 1)
+        weigh(3, 2)
+        back(3, 2)
 
         g_b = sbuf("g_b", [P, D, L], BF16)
         g_q = sbuf("g_q", [P, D], U32)

@@ -21,11 +21,16 @@ TANH = mybir.ActivationFunctionType.Tanh
 
 P = 128
 L = 4
+LAST = L - 1
+PAIR = 2
+RUN = 4
+QUADRANT = 32
 
 
 def tile_attend_glch_pl_x_ts_kernel(tc, xT, wT, y, wt, ts, offs, out_0, out_1, out_2):
     nc = tc.nc
     lanes = range(L)
+    pairs = range(L // PAIR)
     with ExitStack() as ctx:
         sb = ctx.enter_context(tc.tile_pool(name="sb", bufs=1))
         ps = ctx.enter_context(tc.psum_pool(name="ps", bufs=1))
@@ -38,10 +43,6 @@ def tile_attend_glch_pl_x_ts_kernel(tc, xT, wT, y, wt, ts, offs, out_0, out_1, o
         ts_win = sbuf("ts_win", [P, T], F32)
         nc.vector.memset(ts_win[:, : T // 2], 0.0)
         nc.gpsimd.memset(ts_win[:, T // 2 :], 0.0)
-        warm = sbuf("warm", [P, 8], F32)
-        nc.vector.memset(warm[:], 0.0)
-        warm_out = sbuf("warm_out", [P, 8], F32)
-        nc.scalar.activation(warm_out[:], warm[:], TANH)
 
         x_raw = sbuf("x_raw", [P, L, R], F32)
         nc.sync.dma_start(x_raw[:], xT[0].rearrange("(p j) r -> p j r", j=L))
@@ -52,14 +53,15 @@ def tile_attend_glch_pl_x_ts_kernel(tc, xT, wT, y, wt, ts, offs, out_0, out_1, o
         w_rows = wT.rearrange("(p j) c -> p j c", j=L)
         y_rows = y[0].rearrange("(m t) i -> m t i", t=L)
         w_win = [sbuf("w_win%d" % j, [P, T], F32) for j in lanes]
-        y_early = sbuf("y_early", [P, 2, N], F32)
-        y_late = [sbuf("y_late%d" % k, [P, N], F32) for k in range(2)]
+        y_early = sbuf("y_early", [P, PAIR, N], F32)
+        y_late = [sbuf("y_late%d" % e, [P, N], F32) for e in range(PAIR)]
+        y_raw = [y_early[:, e] for e in range(PAIR)] + [tile[:] for tile in y_late]
         for j in lanes:
             nc.sync.dma_start(w_win[j][:], w_rows[:, j, :])
-            if j == 1:
-                nc.sync.dma_start(y_early[:], y_rows[:, 0:2, :])
-            if j >= 2:
-                nc.sync.dma_start(y_late[j - 2][:], y_rows[:, j, :])
+            if j == PAIR - 1:
+                nc.sync.dma_start(y_early[:], y_rows[:, 0:PAIR, :])
+            if j >= PAIR:
+                nc.sync.dma_start(y_raw[j], y_rows[:, j, :])
 
         ident_f = sbuf("ident_f", [P, P], F32)
         make_identity(nc, ident_f[:])
@@ -95,30 +97,30 @@ def tile_attend_glch_pl_x_ts_kernel(tc, xT, wT, y, wt, ts, offs, out_0, out_1, o
             )
 
         w_b = sbuf("w_b", [P, L, P, L], BF16)
-        w_early = sbuf("w_early", [P, (L - 1) * N], BF16)
+        w_early = sbuf("w_early", [P, LAST * N], BF16)
         w_last = sbuf("w_last", [P, N], BF16)
-        w_flat = [w_early[:, j * N : (j + 1) * N] for j in range(L - 1)] + [w_last[:]]
+        w_flat = [w_early[:, j * N : (j + 1) * N] for j in range(LAST)] + [w_last[:]]
         v_b = sbuf("v_b", [P, L * N], BF16)
-        y_t = [sbuf("y_t%d" % u, [P, L, 2, P], F32) for u in range(2)]
+        y_t = [sbuf("y_t%d" % u, [P, L, PAIR, P], F32) for u in pairs]
 
         def gather(j):
             nc.vector.tensor_copy(w_flat[j], w_win[j][:].indirect(offsets[:]))
 
         def turn_w(j, bank):
-            w_ps = ps.tile([P, 2, P], F32, name="w_ps%d" % j, tag=bank)
+            w_ps = ps.tile([P, PAIR, P], F32, name="w_ps%d" % j, tag=bank)
             words = w_flat[j].bitcast(F32)
-            for u in range(2):
-                nc.tensor.transpose(w_ps[:, u, :], words[:, u::2], ident_f[:])
+            for v in pairs:
+                nc.tensor.transpose(w_ps[:, v, :], words[:, v::PAIR], ident_f[:])
             nc.scalar.copy(
-                v_b[:, j * N : (j + 1) * N].bitcast(F32).rearrange("m (p u) -> m p u", u=2),
-                w_ps[:].rearrange("m u p -> m p u"),
+                v_b[:, j * N : (j + 1) * N].bitcast(F32).rearrange("m (p v) -> m p v", v=PAIR),
+                w_ps[:].rearrange("m v p -> m p v"),
             )
 
-        def turn_y(t, bank, slot_lanes):
+        def turn_y(t, bank):
             y_ps = ps.tile([P, L, P], F32, name="y_ps%d" % t, tag=bank)
             for s in lanes:
-                nc.tensor.transpose(y_ps[:, s, :], slot_lanes[s], ident_f[:])
-            nc.scalar.copy(y_t[t // 2][:, :, t % 2, :], y_ps[:])
+                nc.tensor.transpose(y_ps[:, s, :], y_raw[t][:, s::L], ident_f[:])
+            nc.scalar.copy(y_t[t // PAIR][:, :, t % PAIR, :], y_ps[:])
 
         gather(0)
         turn_w(0, "turn_b")
@@ -128,38 +130,41 @@ def tile_attend_glch_pl_x_ts_kernel(tc, xT, wT, y, wt, ts, offs, out_0, out_1, o
         turn_w(1, "turn_a")
         make_factor(2)
         make_factor(3)
-        turn_y(0, "turn_b", [y_early[:, 0, s::L] for s in lanes])
-        turn_y(1, "turn_a", [y_early[:, 1, s::L] for s in lanes])
+        turn_y(0, "turn_b")
+        turn_y(1, "turn_a")
         gather(2)
         turn_w(2, "turn_b")
         w_to = w_b[:].rearrange("p s m j -> p m j s")
-        nc.vector.tensor_copy(w_to[:, :, 0 : L - 1], w_early[:].rearrange("p (j m s) -> p m j s", j=L - 1, s=L))
-        turn_y(2, "turn_a", [y_late[0][:, s::L] for s in lanes])
-        turn_y(3, "turn_b", [y_late[1][:, s::L] for s in lanes])
-        gather(L - 1)
-        v_q = sbuf("v_q", [P, D], U32, tag="w_win3")
+        nc.vector.tensor_copy(w_to[:, :, 0:LAST], w_early[:].rearrange("p (j m s) -> p m j s", j=LAST, s=L))
+        turn_y(2, "turn_a")
+        turn_y(3, "turn_b")
+        gather(LAST)
+        v_q = sbuf("v_q", [P, D], U32, tag="w_win%d" % LAST)
         v_s = sbuf("v_s", [P, D], U8)
 
-        def quant_v(half):
-            cols = slice(half * D // 2, (half + 1) * D // 2)
-            nc.vector.quantize_mx(v_q[:, cols].bitcast(E4M3), v_s[:, cols], v_b[:, 2 * half * N : 2 * (half + 1) * N])
+        def quant_v(first_j):
+            cols = slice(first_j * P, (first_j + PAIR) * P)
+            nc.vector.quantize_mx(v_q[:, cols].bitcast(E4M3), v_s[:, cols], v_b[:, first_j * N : (first_j + PAIR) * N])
 
         quant_v(0)
-        turn_w(L - 1, "turn_c")
+        turn_w(LAST, "turn_c")
         w_q = sbuf("w_q", [P, N], U32)
         w_s = sbuf("w_s", [P, N], U8)
         last_from = w_last[:].rearrange("p (m s) -> p m s", s=L)
-        for v in range(2):
-            nc.vector.tensor_copy(w_to[:, :, L - 1, 2 * v : 2 * v + 2], last_from[:, :, 2 * v : 2 * v + 2])
+        for v in pairs:
+            slot_lanes = slice(PAIR * v, PAIR * (v + 1))
+            nc.vector.tensor_copy(w_to[:, :, LAST, slot_lanes], last_from[:, :, slot_lanes])
         for s in lanes:
             slots = slice(s * P, (s + 1) * P)
             nc.vector.quantize_mx(w_q[:, slots].bitcast(E4M3), w_s[:, slots], w_b[:, s].rearrange("p m j -> p (m j)"))
 
-        first = [ps.tile([P, 2 * P], F32, name="score0%d" % s, tag="mx%d" % s) for s in lanes]
-        second = [ps.tile([P, 2, 2 * P], F32, name="score1%d" % v, tag=("wt_ps", "turn_a")[v]) for v in range(2)]
-        score = [[first[s][:] for s in lanes], [second[s // 2][:, s % 2, :] for s in lanes]]
-        for u in range(2):
-            rows = slice(u * 2 * P, (u + 1) * 2 * P)
+        first_banks = [ps.tile([P, PAIR * P], F32, name="score0%d" % s, tag="mx%d" % s) for s in lanes]
+        second_banks = [
+            ps.tile([P, PAIR, PAIR * P], F32, name="score1%d" % v, tag=("wt_ps", "turn_a")[v]) for v in pairs
+        ]
+        score = [[first_banks[s][:] for s in lanes], [second_banks[s // PAIR][:, s % PAIR, :] for s in lanes]]
+        for u in pairs:
+            rows = slice(u * PAIR * P, (u + 1) * PAIR * P)
             for s in lanes:
                 slots = slice(s * P, (s + 1) * P)
                 nc.tensor.matmul_mx(
@@ -172,7 +177,7 @@ def tile_attend_glch_pl_x_ts_kernel(tc, xT, wT, y, wt, ts, offs, out_0, out_1, o
                     stop=True,
                 )
 
-        z = [sbuf("z%d" % u, [P, L, 2, P], F32) for u in range(2)]
+        z = [sbuf("z%d" % u, [P, L, PAIR, P], F32) for u in pairs]
         th = [sbuf("th%d" % t, [P, P, L], F32) for t in lanes]
         h_b = [sbuf("h_b%d" % t, [P, P * L], BF16) for t in lanes]
         h_q = [sbuf("h_q%d" % t, [P, P], U32) for t in lanes]
@@ -190,26 +195,26 @@ def tile_attend_glch_pl_x_ts_kernel(tc, xT, wT, y, wt, ts, offs, out_0, out_1, o
                     MULT,
                     SUB,
                 )
-            for e in range(2):
+            for e in range(PAIR):
                 nc.scalar.activation(
-                    th[2 * u + e][:].rearrange("p (c i) s -> p c s i", i=L),
-                    z[u][:, :, e, :].rearrange("p s (c i) -> p c s i", i=L),
+                    th[PAIR * u + e][:].rearrange("p (c n) s -> p c s n", n=RUN),
+                    z[u][:, :, e, :].rearrange("p s (c n) -> p c s n", n=RUN),
                     TANH,
                 )
 
         def weigh(t, parts):
             for k in range(parts):
-                rows = slice(k * P // parts, (k + 1) * P // parts)
+                ms = slice(k * P // parts, (k + 1) * P // parts)
                 nc.vector.tensor_tensor(
-                    h_b[t][:].rearrange("p (m s) -> p m s", s=L)[:, rows], th[t][:, rows], factor[t][:, rows], MULT
+                    h_b[t][:].rearrange("p (m s) -> p m s", s=L)[:, ms], th[t][:, ms], factor[t][:, ms], MULT
                 )
 
         def back(t, parts):
             for k in range(parts):
-                rows = slice(k * P // parts, (k + 1) * P // parts)
+                ms = slice(k * P // parts, (k + 1) * P // parts)
                 nc.vector.quantize_mx(
-                    h_q[t][:, rows].bitcast(E5M2),
-                    h_s[t][:, rows],
+                    h_q[t][:, ms].bitcast(E5M2),
+                    h_s[t][:, ms],
                     h_b[t][:, k * P * L // parts : (k + 1) * P * L // parts],
                 )
             acc = ps.tile([P, L, P], F32, name="acc%d" % t, tag="mx%d" % t)
@@ -231,28 +236,28 @@ def tile_attend_glch_pl_x_ts_kernel(tc, xT, wT, y, wt, ts, offs, out_0, out_1, o
             nc.sync.dma_start(out_rows[:, t, :], g[:, t * D : (t + 1) * D])
 
         residual(0)
-        quant_v(1)
+        quant_v(PAIR)
         residual(1)
-        weigh(0, 1)
-        weigh(1, 1)
-        back(0, 1)
-        weigh(2, 1)
-        back(1, 1)
-        back(2, 1)
-        weigh(3, 2)
-        back(3, 2)
+        weigh(0, parts=1)
+        weigh(1, parts=1)
+        back(0, parts=1)
+        weigh(2, parts=1)
+        back(1, parts=1)
+        back(2, parts=1)
+        weigh(LAST, parts=2)
+        back(LAST, parts=2)
 
         g_b = sbuf("g_b", [P, D, L], BF16)
         g_q = sbuf("g_q", [P, D], U32)
         g_s = sbuf("g_s", [P, D], U8)
-        g_from = g[:].rearrange("p (t c i) -> p c t i", t=L, i=L)
-        g_to = g_b[:].rearrange("p (c i) t -> p c t i", i=L)
-        nc.vector.tensor_copy(g_to[:, :, 0:2], g_from[:, :, 0:2])
+        g_from = g[:].rearrange("p (t c n) -> p c t n", t=L, n=RUN)
+        g_to = g_b[:].rearrange("p (c n) t -> p c t n", n=RUN)
+        nc.vector.tensor_copy(g_to[:, :, 0:PAIR], g_from[:, :, 0:PAIR])
         half = D // 2
         words_out = out_1[0].rearrange("p d l -> p (d l)").bitcast(I32)
         for k in range(2):
-            runs = slice(k * half // L, (k + 1) * half // L)
-            nc.vector.tensor_copy(g_to[:, runs, 2:L], g_from[:, runs, 2:L])
+            runs = slice(k * half // RUN, (k + 1) * half // RUN)
+            nc.vector.tensor_copy(g_to[:, runs, PAIR:L], g_from[:, runs, PAIR:L])
         for k in range(2):
             cols = slice(k * half, (k + 1) * half)
             nc.vector.quantize_mx(
@@ -260,6 +265,6 @@ def tile_attend_glch_pl_x_ts_kernel(tc, xT, wT, y, wt, ts, offs, out_0, out_1, o
             )
             nc.sync.dma_start(words_out[:, cols], g_q[:, cols].bitcast(I32))
         scale_rows = out_2[0].bitcast(I32)
-        for q in lanes:
-            eng = nc.scalar if q % 2 == 0 else nc.sync
-            eng.dma_start(scale_rows[L * q : L * (q + 1), :], g_s[32 * q : 32 * q + L, :].bitcast(I32))
+        for q in range(P // QUADRANT):
+            queue = nc.scalar if q % 2 == 0 else nc.sync
+            queue.dma_start(scale_rows[L * q : L * (q + 1), :], g_s[QUADRANT * q : QUADRANT * q + L, :].bitcast(I32))

@@ -17,6 +17,7 @@ E4M3 = mybir.dt.float8_e4m3fn_x4
 E5M2 = mybir.dt.float8_e5m2_x4
 MULT = mybir.AluOpType.mult
 SUB = mybir.AluOpType.subtract
+COPY = mybir.ActivationFunctionType.Copy
 TANH = mybir.ActivationFunctionType.Tanh
 
 P = 128
@@ -45,23 +46,23 @@ def tile_attend_glch_pl_x_ts_kernel(tc, xT, wT, y, wt, ts, offs, out_0, out_1, o
         nc.gpsimd.memset(ts_win[:, T // 2 :], 0.0)
 
         x_raw = sbuf("x_raw", [P, L, R], F32)
-        nc.sync.dma_start(x_raw[:], xT[0].rearrange("(p j) r -> p j r", j=L))
+        w_rows = wT.rearrange("(p j) c -> p j c", j=L)
+        w_win = [sbuf("w_win%d" % j, [P, T], F32) for j in lanes]
+        nc.sync.dma_start(w_win[0][:], w_rows[:, 0, :])
         nc.sync.dma_start(offsets[:], offs)
         wt_col = sbuf("wt_col", [P, L], F32)
         nc.sync.dma_start(wt_col[:], wt[0].rearrange("(m t) o -> m (t o)", t=L))
         nc.sync.dma_start(ts_win[0:1, :], ts[0:1, :])
-        w_rows = wT.rearrange("(p j) c -> p j c", j=L)
         y_rows = y[0].rearrange("(m t) i -> m t i", t=L)
-        w_win = [sbuf("w_win%d" % j, [P, T], F32) for j in lanes]
-        y_early = sbuf("y_early", [P, PAIR, N], F32)
-        y_late = [sbuf("y_late%d" % e, [P, N], F32) for e in range(PAIR)]
-        y_raw = [y_early[:, e] for e in range(PAIR)] + [tile[:] for tile in y_late]
-        for j in lanes:
+        y_one = [sbuf("y_one%d" % e, [P, N], F32) for e in range(PAIR)]
+        y_two = sbuf("y_two", [P, PAIR, N], F32)
+        y_raw = [tile[:] for tile in y_one] + [y_two[:, e] for e in range(PAIR)]
+        for j in range(1, L):
             nc.sync.dma_start(w_win[j][:], w_rows[:, j, :])
-            if j == PAIR - 1:
-                nc.sync.dma_start(y_early[:], y_rows[:, 0:PAIR, :])
-            if j >= PAIR:
-                nc.sync.dma_start(y_raw[j], y_rows[:, j, :])
+            if j % PAIR == 1:
+                nc.sync.dma_start(y_raw[j // PAIR], y_rows[:, j // PAIR, :])
+        nc.sync.dma_start(y_two[:], y_rows[:, PAIR:L, :])
+        nc.sync.dma_start(x_raw[:], xT[0].rearrange("(p j) r -> p j r", j=L))
 
         ident_f = sbuf("ident_f", [P, P], F32)
         make_identity(nc, ident_f[:])
@@ -70,97 +71,121 @@ def tile_attend_glch_pl_x_ts_kernel(tc, xT, wT, y, wt, ts, offs, out_0, out_1, o
         for t in lanes:
             nc.tensor.transpose(wt_ps[:, t, :], wt_col[:, t : t + 1].to_broadcast([P, P]), ident_f[:])
 
-        x_b = sbuf("x_b", [P, L, P, L], BF16)
-        x_to = x_b[:].rearrange("p t m j -> p m j t")
-        x_from = x_raw[:].rearrange("p j (m t) -> p m j t", t=L)
-        nc.vector.tensor_copy(x_to[:, : P // 2], x_from[:, : P // 2])
-        nc.scalar.copy(x_to[:, P // 2 :], x_from[:, P // 2 :])
         ts_g = sbuf("ts_g", [P, N], F32)
         nc.vector.tensor_copy(ts_g[:], ts_win[:].indirect(offsets[:]))
         x_q = sbuf("x_q", [P, R], U32)
         x_s = sbuf("x_s", [P, R], U8)
-        nc.vector.quantize_mx(x_q[:].bitcast(E4M3), x_s[:], x_b[:].rearrange("p t m j -> p (t m j)"))
 
         ts_ps = ps.tile([P, L, P], F32, name="ts_ps", tag="turn_a")
         for s in lanes:
             nc.tensor.transpose(ts_ps[:, s, :], ts_g[:, s::L], ident_f[:])
         ts_col = sbuf("ts_col", [P, L], F32)
         nc.scalar.copy(ts_col[:], ts_ps[:, :, 0])
-        factor = [sbuf("factor%d" % t, [P, P, L], F32) for t in lanes]
 
         def make_factor(t):
             nc.vector.tensor_tensor(
-                factor[t][:],
+                factor[t],
                 wt_ps[:, t, :].unsqueeze(2).broadcast_to([P, P, L]),
                 ts_col[:].unsqueeze(1).broadcast_to([P, P, L]),
                 MULT,
             )
 
-        w_b = sbuf("w_b", [P, L, P, L], BF16)
-        w_early = sbuf("w_early", [P, LAST * N], BF16)
-        w_last = sbuf("w_last", [P, N], BF16)
-        w_flat = [w_early[:, j * N : (j + 1) * N] for j in range(LAST)] + [w_last[:]]
+        w_b = [sbuf("w_b%d" % v, [P, PAIR, P, L], BF16) for v in pairs]
+        w_all = sbuf("w_all", [P, L * N], BF16, tag="ts_win")
+        w_flat = [w_all[:, j * N : (j + 1) * N] for j in lanes]
         v_b = sbuf("v_b", [P, L * N], BF16)
-        y_t = [sbuf("y_t%d" % u, [P, L, PAIR, P], F32) for u in pairs]
+        y_t = [sbuf("y_t0", [P, L, PAIR, P], F32)]
 
         def gather(j):
             nc.vector.tensor_copy(w_flat[j], w_win[j][:].indirect(offsets[:]))
 
         def turn_w(j, bank):
-            w_ps = ps.tile([P, PAIR, P], F32, name="w_ps%d" % j, tag=bank)
+            w_one = ps.tile([P, PAIR, P], F32, name="w_ps%d" % j, tag=bank)
+            w_ps = w_one[:]
             words = w_flat[j].bitcast(F32)
             for v in pairs:
                 nc.tensor.transpose(w_ps[:, v, :], words[:, v::PAIR], ident_f[:])
             nc.scalar.copy(
                 v_b[:, j * N : (j + 1) * N].bitcast(F32).rearrange("m (p v) -> m p v", v=PAIR),
-                w_ps[:].rearrange("m v p -> m p v"),
+                w_ps.rearrange("m v p -> m p v"),
             )
 
-        def turn_y(t, bank):
-            y_ps = ps.tile([P, L, P], F32, name="y_ps%d" % t, tag=bank)
+        def turn_y(t, y_ps):
             for s in lanes:
                 nc.tensor.transpose(y_ps[:, s, :], y_raw[t][:, s::L], ident_f[:])
-            nc.scalar.copy(y_t[t // PAIR][:, :, t % PAIR, :], y_ps[:])
 
-        gather(0)
-        turn_w(0, "turn_b")
-        make_factor(0)
-        make_factor(1)
-        gather(1)
-        turn_w(1, "turn_a")
-        make_factor(2)
-        make_factor(3)
-        turn_y(0, "turn_b")
-        turn_y(1, "turn_a")
-        gather(2)
-        turn_w(2, "turn_b")
-        w_to = w_b[:].rearrange("p s m j -> p m j s")
-        nc.vector.tensor_copy(w_to[:, :, 0:LAST], w_early[:].rearrange("p (j m s) -> p m j s", j=LAST, s=L))
-        turn_y(2, "turn_a")
-        turn_y(3, "turn_b")
-        gather(LAST)
-        v_q = sbuf("v_q", [P, D], U32, tag="w_win%d" % LAST)
+        def copy_y(t, y_ps):
+            nc.scalar.copy(y_t[t // PAIR][:, :, t % PAIR, :], y_ps)
+
         v_s = sbuf("v_s", [P, D], U8)
+        w_q = sbuf("w_q", [P, N], U32)
+        w_s = sbuf("w_s", [P, N], U8)
 
         def quant_v(first_j):
             cols = slice(first_j * P, (first_j + PAIR) * P)
             nc.vector.quantize_mx(v_q[:, cols].bitcast(E4M3), v_s[:, cols], v_b[:, first_j * N : (first_j + PAIR) * N])
 
-        quant_v(0)
-        turn_w(LAST, "turn_c")
-        w_q = sbuf("w_q", [P, N], U32)
-        w_s = sbuf("w_s", [P, N], U8)
-        last_from = w_last[:].rearrange("p (m s) -> p m s", s=L)
-        for v in pairs:
-            slot_lanes = slice(PAIR * v, PAIR * (v + 1))
-            nc.vector.tensor_copy(w_to[:, :, LAST, slot_lanes], last_from[:, :, slot_lanes])
+        gather(0)
+        turn_w(0, "turn_a")
+        factor_flat = sbuf("factor_flat", [P, L, PAIR, P], F32)
         for s in lanes:
-            slots = slice(s * P, (s + 1) * P)
-            nc.vector.quantize_mx(w_q[:, slots].bitcast(E4M3), w_s[:, slots], w_b[:, s].rearrange("p m j -> p (m j)"))
+            nc.scalar.activation(factor_flat[:, s], wt_ps[:, PAIR:L], COPY, scale=ts_col[:, s : s + 1])
+        y_ps = [ps.tile([P, L, P], F32, name="y_ps0", tag="turn_d")]
+        turn_y(0, y_ps[0][:])
+        copy_y(0, y_ps[0][:])
+        gather(1)
+        turn_w(1, "turn_a")
+        factor_all = sbuf("factor_all", [P, L, P, L], F32, tag="w_win1")
+        factor = [factor_all[:, t] for t in lanes]
+        for t in range(PAIR):
+            make_factor(t)
+        for e in range(PAIR):
+            nc.scalar.copy(
+                factor[PAIR + e].rearrange("p (c n) s -> p c s n", n=RUN),
+                factor_flat[:, :, e, :].rearrange("p s (c n) -> p c s n", n=RUN),
+            )
+        gather(2)
+        turn_w(2, "turn_b")
+        v_q = sbuf("v_q", [P, D], U32, tag="w_win2")
+        quant_v(0)
+        gather(LAST)
+        turn_w(LAST, "turn_c")
+        for v in pairs:
+            nc.vector.tensor_copy(
+                w_b[v][:].rearrange("p s m j -> p m j s"),
+                w_all[:].rearrange("p (j m s) -> p m j s", j=L, s=L)[:, :, :, PAIR * v : PAIR * (v + 1)],
+            )
+        for t in range(1, L):
+            y_ps.append(ps.tile([P, L, P], F32, name="y_ps%d" % t, tag=("turn_c", "turn_b")[t % PAIR]))
+            turn_y(t, y_ps[t][:])
+            if t < PAIR:
+                copy_y(t, y_ps[t][:])
+        for v in pairs:
+            slots = slice(v * PAIR * P, (v + 1) * PAIR * P)
+            nc.vector.quantize_mx(
+                w_q[:, slots].bitcast(E4M3), w_s[:, slots], w_b[v][:].rearrange("p s m j -> p (s m j)")
+            )
+        quant_v(PAIR)
 
-        first_banks = [ps.tile([P, PAIR * P], F32, name="score0%d" % s, tag="mx%d" % s) for s in lanes]
+        x_b = [sbuf("x_b%d" % u, [P, PAIR, P, L], BF16, tag=("w_b1", "ts_win")[u]) for u in pairs]
+        for u in pairs:
+            (nc.vector.tensor_copy, nc.scalar.copy)[u](
+                x_b[u][:].rearrange("p t m j -> p m j t"),
+                x_raw[:].rearrange("p j (m t) -> p m j t", t=L)[:, :, :, PAIR * u : PAIR * (u + 1)],
+            )
+        for u in pairs:
+            rows = slice(u * PAIR * P, (u + 1) * PAIR * P)
+            nc.vector.quantize_mx(
+                x_q[:, rows].bitcast(E4M3), x_s[:, rows], x_b[u][:].rearrange("p t m j -> p (t m j)")
+            )
+        y_t.append(sbuf("y_t1", [P, L, PAIR, P], F32, tag="x_raw"))
+        for e in range(PAIR):
+            copy_y(PAIR + e, y_ps[PAIR + e][:])
+
+        mx_banks = ("mx0", "mx1", "mx2", "turn_a")
+        first_banks = [ps.tile([P, PAIR * P], F32, name="score0%d" % s, tag=mx_banks[s]) for s in lanes]
         second_banks = [
-            ps.tile([P, PAIR, PAIR * P], F32, name="score1%d" % v, tag=("wt_ps", "turn_a")[v]) for v in pairs
+            ps.tile([P, PAIR, PAIR * P], F32, name="score1%d" % v, tag=("wt_ps", "turn_d")[v]) for v in pairs
         ]
         score = [[first_banks[s][:] for s in lanes], [second_banks[s // PAIR][:, s % PAIR, :] for s in lanes]]
         for u in pairs:
@@ -217,7 +242,7 @@ def tile_attend_glch_pl_x_ts_kernel(tc, xT, wT, y, wt, ts, offs, out_0, out_1, o
                     h_s[t][:, ms],
                     h_b[t][:, k * P * L // parts : (k + 1) * P * L // parts],
                 )
-            acc = ps.tile([P, L, P], F32, name="acc%d" % t, tag="mx%d" % t)
+            acc = ps.tile([P, L, P], F32, name="acc%d" % t, tag=mx_banks[t])
             nc.tensor.matmul_mx(
                 acc[:].rearrange("m j p -> m (j p)"),
                 lhsT=h_q[t][:].bitcast(E5M2),
@@ -236,7 +261,6 @@ def tile_attend_glch_pl_x_ts_kernel(tc, xT, wT, y, wt, ts, offs, out_0, out_1, o
             nc.sync.dma_start(out_rows[:, t, :], g[:, t * D : (t + 1) * D])
 
         residual(0)
-        quant_v(PAIR)
         residual(1)
         weigh(0, parts=1)
         weigh(1, parts=1)

@@ -121,15 +121,11 @@ def tile_attend_glch_pl_x_ts_kernel(tc, xT, wT, y, wt, ts, offs, out_0, out_1, o
         w_q = sbuf("w_q", [P, N], U32)
         w_s = sbuf("w_s", [P, N], U8)
 
-        def quant_v(first_j):
-            cols = slice(first_j * P, (first_j + PAIR) * P)
-            nc.vector.quantize_mx(v_q[:, cols].bitcast(E4M3), v_s[:, cols], v_b[:, first_j * N : (first_j + PAIR) * N])
-
         gather(0)
         turn_w(0, "turn_a")
-        factor_flat = sbuf("factor_flat", [P, L, PAIR, P], F32)
+        factor_flat = sbuf("factor_flat", [P, L, LAST, P], F32)
         for s in lanes:
-            nc.scalar.activation(factor_flat[:, s], wt_ps[:, PAIR:L], COPY, scale=ts_col[:, s : s + 1])
+            nc.scalar.activation(factor_flat[:, s], wt_ps[:, 1:L], COPY, scale=ts_col[:, s : s + 1])
         y_ps = [ps.tile([P, L, P], F32, name="y_ps0", tag="turn_d")]
         turn_y(0, y_ps[0][:])
         copy_y(0, y_ps[0][:])
@@ -137,17 +133,14 @@ def tile_attend_glch_pl_x_ts_kernel(tc, xT, wT, y, wt, ts, offs, out_0, out_1, o
         turn_w(1, "turn_a")
         factor_all = sbuf("factor_all", [P, L, P, L], F32, tag="w_win1")
         factor = [factor_all[:, t] for t in lanes]
-        for t in range(PAIR):
-            make_factor(t)
-        for e in range(PAIR):
+        make_factor(0)
+        for e in range(LAST):
             nc.scalar.copy(
-                factor[PAIR + e].rearrange("p (c n) s -> p c s n", n=RUN),
+                factor[1 + e].rearrange("p (c n) s -> p c s n", n=RUN),
                 factor_flat[:, :, e, :].rearrange("p s (c n) -> p c s n", n=RUN),
             )
         gather(2)
         turn_w(2, "turn_b")
-        v_q = sbuf("v_q", [P, D], U32, tag="w_win2")
-        quant_v(0)
         gather(LAST)
         turn_w(LAST, "turn_c")
         for v in pairs:
@@ -165,7 +158,9 @@ def tile_attend_glch_pl_x_ts_kernel(tc, xT, wT, y, wt, ts, offs, out_0, out_1, o
             nc.vector.quantize_mx(
                 w_q[:, slots].bitcast(E4M3), w_s[:, slots], w_b[v][:].rearrange("p s m j -> p (s m j)")
             )
-        quant_v(PAIR)
+
+        v_q = sbuf("v_q", [P, D], U32, tag="w_b0")
+        nc.vector.quantize_mx(v_q[:].bitcast(E4M3), v_s[:], v_b[:])
 
         x_b = [sbuf("x_b%d" % u, [P, PAIR, P, L], BF16, tag=("w_b1", "ts_win")[u]) for u in pairs]
         for u in pairs:

@@ -25,6 +25,7 @@ L = 4
 LAST = L - 1
 PAIR = 2
 RUN = 4
+X_SPLIT = 5 * P // 8
 QUADRANT = 32
 
 
@@ -82,14 +83,6 @@ def tile_attend_glch_pl_x_ts_kernel(tc, xT, wT, y, wt, ts, offs, out_0, out_1, o
         ts_col = sbuf("ts_col", [P, L], F32)
         nc.scalar.copy(ts_col[:], ts_ps[:, :, 0])
 
-        def make_factor(t):
-            nc.vector.tensor_tensor(
-                factor[t],
-                wt_ps[:, t, :].unsqueeze(2).broadcast_to([P, P, L]),
-                ts_col[:].unsqueeze(1).broadcast_to([P, P, L]),
-                MULT,
-            )
-
         w_b = [sbuf("w_b%d" % v, [P, PAIR, P, L], BF16) for v in pairs]
         w_all = sbuf("w_all", [P, L * N], BF16, tag="ts_win")
         w_flat = [w_all[:, j * N : (j + 1) * N] for j in lanes]
@@ -100,22 +93,21 @@ def tile_attend_glch_pl_x_ts_kernel(tc, xT, wT, y, wt, ts, offs, out_0, out_1, o
             nc.vector.tensor_copy(w_flat[j], w_win[j][:].indirect(offsets[:]))
 
         def turn_w(j, bank):
-            w_one = ps.tile([P, PAIR, P], F32, name="w_ps%d" % j, tag=bank)
-            w_ps = w_one[:]
+            w_ps = ps.tile([P, PAIR, P], F32, name="w_ps%d" % j, tag=bank)
             words = w_flat[j].bitcast(F32)
             for v in pairs:
                 nc.tensor.transpose(w_ps[:, v, :], words[:, v::PAIR], ident_f[:])
             nc.scalar.copy(
                 v_b[:, j * N : (j + 1) * N].bitcast(F32).rearrange("m (p v) -> m p v", v=PAIR),
-                w_ps.rearrange("m v p -> m p v"),
+                w_ps[:].rearrange("m v p -> m p v"),
             )
 
-        def turn_y(t, y_ps):
+        def turn_y(t):
             for s in lanes:
-                nc.tensor.transpose(y_ps[:, s, :], y_raw[t][:, s::L], ident_f[:])
+                nc.tensor.transpose(y_ps[t][:, s, :], y_raw[t][:, s::L], ident_f[:])
 
-        def copy_y(t, y_ps):
-            nc.scalar.copy(y_t[t // PAIR][:, :, t % PAIR, :], y_ps)
+        def copy_y(t):
+            nc.scalar.copy(y_t[t // PAIR][:, :, t % PAIR, :], y_ps[t][:])
 
         v_s = sbuf("v_s", [P, D], U8)
         w_q = sbuf("w_q", [P, N], U32)
@@ -127,17 +119,22 @@ def tile_attend_glch_pl_x_ts_kernel(tc, xT, wT, y, wt, ts, offs, out_0, out_1, o
         for s in lanes:
             nc.scalar.activation(factor_flat[:, s], wt_ps[:, 1:L], COPY, scale=ts_col[:, s : s + 1])
         y_ps = [ps.tile([P, L, P], F32, name="y_ps0", tag="turn_d")]
-        turn_y(0, y_ps[0][:])
-        copy_y(0, y_ps[0][:])
+        turn_y(0)
+        copy_y(0)
         gather(1)
         turn_w(1, "turn_a")
         factor_all = sbuf("factor_all", [P, L, P, L], F32, tag="w_win1")
         factor = [factor_all[:, t] for t in lanes]
-        make_factor(0)
-        for e in range(LAST):
+        nc.vector.tensor_tensor(
+            factor[0],
+            wt_ps[:, 0, :].unsqueeze(2).broadcast_to([P, P, L]),
+            ts_col[:].unsqueeze(1).broadcast_to([P, P, L]),
+            MULT,
+        )
+        for t in range(1, L):
             nc.scalar.copy(
-                factor[1 + e].rearrange("p (c n) s -> p c s n", n=RUN),
-                factor_flat[:, :, e, :].rearrange("p s (c n) -> p c s n", n=RUN),
+                factor[t].rearrange("p (c n) s -> p c s n", n=RUN),
+                factor_flat[:, :, t - 1, :].rearrange("p s (c n) -> p c s n", n=RUN),
             )
         gather(2)
         turn_w(2, "turn_b")
@@ -150,9 +147,9 @@ def tile_attend_glch_pl_x_ts_kernel(tc, xT, wT, y, wt, ts, offs, out_0, out_1, o
             )
         for t in range(1, L):
             y_ps.append(ps.tile([P, L, P], F32, name="y_ps%d" % t, tag=("turn_c", "turn_b")[t % PAIR]))
-            turn_y(t, y_ps[t][:])
+            turn_y(t)
             if t < PAIR:
-                copy_y(t, y_ps[t][:])
+                copy_y(t)
         for v in pairs:
             slots = slice(v * PAIR * P, (v + 1) * PAIR * P)
             nc.vector.quantize_mx(
@@ -162,20 +159,20 @@ def tile_attend_glch_pl_x_ts_kernel(tc, xT, wT, y, wt, ts, offs, out_0, out_1, o
         v_q = sbuf("v_q", [P, D], U32, tag="w_b0")
         nc.vector.quantize_mx(v_q[:].bitcast(E4M3), v_s[:], v_b[:])
 
-        x_b = [sbuf("x_b%d" % u, [P, PAIR, P, L], BF16, tag=("w_b1", "ts_win")[u]) for u in pairs]
+        x_b = [sbuf("x_b%d" % u, [P, PAIR, P, L], BF16, tag=("ts_win", "w_b1")[u]) for u in pairs]
         for u in pairs:
-            (nc.vector.tensor_copy, nc.scalar.copy)[u](
-                x_b[u][:].rearrange("p t m j -> p m j t"),
-                x_raw[:].rearrange("p j (m t) -> p m j t", t=L)[:, :, :, PAIR * u : PAIR * (u + 1)],
-            )
+            x_to = x_b[u][:].rearrange("p t m j -> p m j t")
+            x_from = x_raw[:].rearrange("p j (m t) -> p m j t", t=L)[:, :, :, PAIR * u : PAIR * (u + 1)]
+            nc.vector.tensor_copy(x_to[:, :X_SPLIT], x_from[:, :X_SPLIT])
+            nc.scalar.copy(x_to[:, X_SPLIT:], x_from[:, X_SPLIT:])
         for u in pairs:
             rows = slice(u * PAIR * P, (u + 1) * PAIR * P)
             nc.vector.quantize_mx(
                 x_q[:, rows].bitcast(E4M3), x_s[:, rows], x_b[u][:].rearrange("p t m j -> p (t m j)")
             )
         y_t.append(sbuf("y_t1", [P, L, PAIR, P], F32, tag="x_raw"))
-        for e in range(PAIR):
-            copy_y(PAIR + e, y_ps[PAIR + e][:])
+        for t in range(PAIR, L):
+            copy_y(t)
 
         mx_banks = ("mx0", "mx1", "mx2", "turn_a")
         first_banks = [ps.tile([P, PAIR * P], F32, name="score0%d" % s, tag=mx_banks[s]) for s in lanes]

@@ -86,7 +86,7 @@ def tile_attend_glch_pl_x_ts_kernel(tc, xT, wT, y, wt, ts, offs, out_0, out_1, o
         w_b = [sbuf("w_b%d" % v, [P, PAIR, P, L], BF16) for v in pairs]
         w_all = sbuf("w_all", [P, L * N], BF16, tag="ts_win")
         w_flat = [w_all[:, j * N : (j + 1) * N] for j in lanes]
-        v_b = sbuf("v_b", [P, L * N], BF16)
+        v_b = [sbuf("v_b%d" % u, [P, PAIR * N], BF16) for u in pairs]
         y_t = [sbuf("y_t0", [P, L, PAIR, P], F32)]
 
         def gather(j):
@@ -98,7 +98,7 @@ def tile_attend_glch_pl_x_ts_kernel(tc, xT, wT, y, wt, ts, offs, out_0, out_1, o
             for v in pairs:
                 nc.tensor.transpose(w_ps[:, v, :], words[:, v::PAIR], ident_f[:])
             nc.scalar.copy(
-                v_b[:, j * N : (j + 1) * N].bitcast(F32).rearrange("m (p v) -> m p v", v=PAIR),
+                v_b[j // PAIR][:, j % PAIR * N : (j % PAIR + 1) * N].bitcast(F32).rearrange("m (p v) -> m p v", v=PAIR),
                 w_ps[:].rearrange("m v p -> m p v"),
             )
 
@@ -140,6 +140,13 @@ def tile_attend_glch_pl_x_ts_kernel(tc, xT, wT, y, wt, ts, offs, out_0, out_1, o
         turn_w(2, "turn_b")
         gather(LAST)
         turn_w(LAST, "turn_c")
+        v_q = sbuf("v_q", [P, D], U32, tag="w_win2")
+
+        def quantise_v(u):
+            cols = slice(u * PAIR * P, (u + 1) * PAIR * P)
+            nc.vector.quantize_mx(v_q[:, cols].bitcast(E4M3), v_s[:, cols], v_b[u][:])
+
+        quantise_v(0)
         for v in pairs:
             nc.vector.tensor_copy(
                 w_b[v][:].rearrange("p s m j -> p m j s"),
@@ -156,8 +163,7 @@ def tile_attend_glch_pl_x_ts_kernel(tc, xT, wT, y, wt, ts, offs, out_0, out_1, o
                 w_q[:, slots].bitcast(E4M3), w_s[:, slots], w_b[v][:].rearrange("p s m j -> p (s m j)")
             )
 
-        v_q = sbuf("v_q", [P, D], U32, tag="w_b0")
-        nc.vector.quantize_mx(v_q[:].bitcast(E4M3), v_s[:], v_b[:])
+        quantise_v(1)
 
         x_b = [sbuf("x_b%d" % u, [P, PAIR, P, L], BF16, tag=("ts_win", "w_b1")[u]) for u in pairs]
         for u in pairs:

@@ -139,7 +139,7 @@ def tile_attend_glch_pl_x_ts_kernel(tc, xT, wT, y, wt, ts, offs, out_0, out_1, o
         gather(2)
         turn_w(2, "turn_b")
         gather(LAST)
-        turn_w(LAST, "turn_c")
+        turn_w(LAST, "turn_d")
         v_q = sbuf("v_q", [P, D], U32, tag="w_win2")
 
         def quantise_v(u):
@@ -152,11 +152,16 @@ def tile_attend_glch_pl_x_ts_kernel(tc, xT, wT, y, wt, ts, offs, out_0, out_1, o
                 w_b[v][:].rearrange("p s m j -> p m j s"),
                 w_all[:].rearrange("p (j m s) -> p m j s", j=L, s=L)[:, :, :, PAIR * v : PAIR * (v + 1)],
             )
-        for t in range(1, L):
-            y_ps.append(ps.tile([P, L, P], F32, name="y_ps%d" % t, tag=("turn_c", "turn_b")[t % PAIR]))
+        y1_ps = [ps.tile([P, PAIR, P], F32, name="y1_ps%d" % v, tag=("turn_b", "turn_c")[v]) for v in pairs]
+        for e in range(PAIR):
+            for v in pairs:
+                nc.tensor.transpose(y1_ps[v][:, e, :], y_raw[1][:, PAIR * v + e :: L], ident_f[:])
+        for v in pairs:
+            nc.scalar.copy(y_t[0][:, PAIR * v : PAIR * (v + 1), 1, :], y1_ps[v][:])
+        y_ps.append(None)
+        for t in range(PAIR, L):
+            y_ps.append(ps.tile([P, L, P], F32, name="y_ps%d" % t, tag=("turn_b", "wt_ps")[t % PAIR]))
             turn_y(t)
-            if t < PAIR:
-                copy_y(t)
         for v in pairs:
             slots = slice(v * PAIR * P, (v + 1) * PAIR * P)
             nc.vector.quantize_mx(
@@ -183,7 +188,7 @@ def tile_attend_glch_pl_x_ts_kernel(tc, xT, wT, y, wt, ts, offs, out_0, out_1, o
         mx_banks = ("mx0", "mx1", "mx2", "turn_a")
         first_banks = [ps.tile([P, PAIR * P], F32, name="score0%d" % s, tag=mx_banks[s]) for s in lanes]
         second_banks = [
-            ps.tile([P, PAIR, PAIR * P], F32, name="score1%d" % v, tag=("wt_ps", "turn_d")[v]) for v in pairs
+            ps.tile([P, PAIR, PAIR * P], F32, name="score1%d" % v, tag=("turn_c", "turn_d")[v]) for v in pairs
         ]
         score = [[first_banks[s][:] for s in lanes], [second_banks[s // PAIR][:, s % PAIR, :] for s in lanes]]
         for u in pairs:

@@ -265,6 +265,17 @@ def tile_attend_glch_pl_x_ts_kernel(tc, xT, wT, y, wt, ts, offs, out_0, out_1, o
 
         residual(0)
         residual(1)
+        for bank in ("turn_c", "turn_d"):
+            warm = ps.tile([P, R], F32, name="warm_" + bank, tag=bank)
+            nc.tensor.matmul_mx(
+                warm[:],
+                lhsT=w_q[:, :P].bitcast(E4M3),
+                lhsT_scale=w_s[:, :P],
+                rhs=x_q[:].bitcast(E4M3),
+                rhs_scale=x_s[:],
+                start=True,
+                stop=True,
+            )
         weigh(0, parts=1)
         weigh(1, parts=1)
         back(0, parts=1)

@@ -265,17 +265,16 @@ def tile_attend_glch_pl_x_ts_kernel(tc, xT, wT, y, wt, ts, offs, out_0, out_1, o
 
         residual(0)
         residual(1)
-        for bank in ("turn_c", "turn_d"):
-            warm = ps.tile([P, R], F32, name="warm_" + bank, tag=bank)
-            nc.tensor.matmul_mx(
-                warm[:],
-                lhsT=w_q[:, :P].bitcast(E4M3),
-                lhsT_scale=w_s[:, :P],
-                rhs=x_q[:].bitcast(E4M3),
-                rhs_scale=x_s[:],
-                start=True,
-                stop=True,
-            )
+        warm = ps.tile([P, R], F32, name="warm", tag="turn_d")
+        nc.tensor.matmul_mx(
+            warm[:],
+            lhsT=w_q[:, :P].bitcast(E4M3),
+            lhsT_scale=w_s[:, :P],
+            rhs=x_q[:].bitcast(E4M3),
+            rhs_scale=x_s[:],
+            start=True,
+            stop=True,
+        )
         weigh(0, parts=1)
         weigh(1, parts=1)
         back(0, parts=1)

@@ -43,8 +43,7 @@ def tile_attend_glch_pl_x_ts_kernel(tc, xT, wT, y, wt, ts, offs, out_0, out_1, o
         offsets = sb.tile([P, N // 16], U16, name="offsets")
 
         ts_win = sbuf("ts_win", [P, T], F32)
-        nc.vector.memset(ts_win[:, : T // 2], 0.0)
-        nc.gpsimd.memset(ts_win[:, T // 2 :], 0.0)
+        nc.vector.memset(ts_win[: P - 1, :], 0.0)
 
         x_raw = sbuf("x_raw", [P, L, R], F32)
         w_rows = wT.rearrange("(p j) c -> p j c", j=L)
@@ -53,7 +52,7 @@ def tile_attend_glch_pl_x_ts_kernel(tc, xT, wT, y, wt, ts, offs, out_0, out_1, o
         nc.sync.dma_start(offsets[:], offs)
         wt_col = sbuf("wt_col", [P, L], F32)
         nc.sync.dma_start(wt_col[:], wt[0].rearrange("(m t) o -> m (t o)", t=L))
-        nc.sync.dma_start(ts_win[0:1, :], ts[0:1, :])
+        nc.sync.dma_start(ts_win[P - 1 : P, :], ts[0:1, :])
         y_rows = y[0].rearrange("(m t) i -> m t i", t=L)
         y_one = [sbuf("y_one%d" % e, [P, N], F32) for e in range(PAIR)]
         y_two = sbuf("y_two", [P, PAIR, N], F32)
@@ -81,7 +80,7 @@ def tile_attend_glch_pl_x_ts_kernel(tc, xT, wT, y, wt, ts, offs, out_0, out_1, o
         for s in lanes:
             nc.tensor.transpose(ts_ps[:, s, :], ts_g[:, s::L], ident_f[:])
         ts_col = sbuf("ts_col", [P, L], F32)
-        nc.scalar.copy(ts_col[:], ts_ps[:, :, 0])
+        nc.scalar.copy(ts_col[:], ts_ps[:, :, P - 1])
 
         w_b = [sbuf("w_b%d" % v, [P, PAIR, P, L], BF16) for v in pairs]
         w_all = sbuf("w_all", [P, L * N], BF16, tag="ts_win")

@@ -229,8 +229,8 @@ def tile_attend_glch_pl_x_ts_kernel(tc, xT, wT, y, wt, ts, offs, out_0, out_1, o
                     TANH,
                 )
 
-        def weigh(t, parts):
-            for k in range(parts):
+        def weigh(t, parts, which=None):
+            for k in range(parts) if which is None else [which]:
                 ms = slice(k * P // parts, (k + 1) * P // parts)
                 nc.vector.tensor_tensor(
                     h_b[t][:].rearrange("p (m s) -> p m s", s=L)[:, ms], th[t][:, ms], factor[t][:, ms], MULT
@@ -277,10 +277,11 @@ def tile_attend_glch_pl_x_ts_kernel(tc, xT, wT, y, wt, ts, offs, out_0, out_1, o
         weigh(0, parts=1)
         weigh(1, parts=1)
         back(0, parts=1)
-        weigh(2, parts=1)
         back(1, parts=1)
+        weigh(2, parts=1)
+        weigh(LAST, parts=2, which=0)
         back(2, parts=1)
-        weigh(LAST, parts=2)
+        weigh(LAST, parts=2, which=1)
         back(LAST, parts=2)
 
         g_b = sbuf("g_b", [P, D, L], BF16)

@@ -54,15 +54,13 @@ def tile_attend_glch_pl_x_ts_kernel(tc, xT, wT, y, wt, ts, offs, out_0, out_1, o
         nc.sync.dma_start(wt_col[:], wt[0].rearrange("(m t) o -> m (t o)", t=L))
         nc.sync.dma_start(ts_win[P - 1 : P, :], ts[0:1, :])
         y_rows = y[0].rearrange("(m t) i -> m t i", t=L)
-        y_one = [sbuf("y_one%d" % e, [P, N], F32) for e in range(PAIR)]
-        y_two = sbuf("y_two", [P, PAIR, N], F32)
-        y_raw = [tile[:] for tile in y_one] + [y_two[:, e] for e in range(PAIR)]
+        y_raw = [sbuf("y_raw%d" % t, [P, N], F32) for t in lanes]
         for j in range(1, L):
             nc.sync.dma_start(w_win[j][:], w_rows[:, j, :])
-            if j % PAIR == 1:
-                nc.sync.dma_start(y_raw[j // PAIR], y_rows[:, j // PAIR, :])
-        nc.sync.dma_start(y_two[:], y_rows[:, PAIR:L, :])
+        for t in range(0, LAST):
+            nc.sync.dma_start(y_raw[t][:], y_rows[:, t, :])
         nc.sync.dma_start(x_raw[:], xT[0].rearrange("(p j) r -> p j r", j=L))
+        nc.sync.dma_start(y_raw[LAST][:], y_rows[:, LAST, :])
 
         ident_f = sbuf("ident_f", [P, P], F32)
         make_identity(nc, ident_f[:])
@@ -86,7 +84,7 @@ def tile_attend_glch_pl_x_ts_kernel(tc, xT, wT, y, wt, ts, offs, out_0, out_1, o
         w_all = sbuf("w_all", [P, L * N], BF16, tag="ts_win")
         w_flat = [w_all[:, j * N : (j + 1) * N] for j in lanes]
         v_b = [sbuf("v_b%d" % u, [P, PAIR * N], BF16) for u in pairs]
-        y_t = [sbuf("y_t0", [P, L, PAIR, P], F32)]
+        y_t = sbuf("y_t", [P, L, PAIR, P], F32)
 
         def gather(j):
             nc.vector.tensor_copy(w_flat[j], w_win[j][:].indirect(offsets[:]))
@@ -101,12 +99,11 @@ def tile_attend_glch_pl_x_ts_kernel(tc, xT, wT, y, wt, ts, offs, out_0, out_1, o
                 w_ps[:].rearrange("m v p -> m p v"),
             )
 
-        def turn_y(t):
+        def turn_y(t, bank):
+            y_ps = ps.tile([P, L, P], F32, name="y_ps%d" % t, tag=bank)
             for s in lanes:
-                nc.tensor.transpose(y_ps[t][:, s, :], y_raw[t][:, s::L], ident_f[:])
-
-        def copy_y(t):
-            nc.scalar.copy(y_t[t // PAIR][:, :, t % PAIR, :], y_ps[t][:])
+                nc.tensor.transpose(y_ps[:, s, :], y_raw[t][:, s::L], ident_f[:])
+            return y_ps
 
         v_s = sbuf("v_s", [P, D], U8)
         w_q = sbuf("w_q", [P, N], U32)
@@ -117,9 +114,11 @@ def tile_attend_glch_pl_x_ts_kernel(tc, xT, wT, y, wt, ts, offs, out_0, out_1, o
         factor_flat = sbuf("factor_flat", [P, L, LAST, P], F32)
         for s in lanes:
             nc.scalar.activation(factor_flat[:, s], wt_ps[:, 1:L], COPY, scale=ts_col[:, s : s + 1])
-        y_ps = [ps.tile([P, L, P], F32, name="y_ps0", tag="turn_d")]
-        turn_y(0)
-        copy_y(0)
+        ts_row_ps = ps.tile([P, L, P], F32, name="ts_row_ps", tag="turn_b")
+        for s in lanes:
+            nc.tensor.transpose(ts_row_ps[:, s, :], ts_col[:, s : s + 1].to_broadcast([P, P]), ident_f[:])
+        ts_neg = sbuf("ts_neg", [P, L, P], F32)
+        nc.scalar.activation(ts_neg[:], ts_row_ps[:], COPY, scale=-1.0)
         gather(1)
         turn_w(1, "turn_a")
         factor_all = sbuf("factor_all", [P, L, P, L], F32, tag="w_win1")
@@ -138,6 +137,8 @@ def tile_attend_glch_pl_x_ts_kernel(tc, xT, wT, y, wt, ts, offs, out_0, out_1, o
         gather(2)
         turn_w(2, "turn_b")
         gather(LAST)
+        nc.scalar.copy(y_t[:, :, 0, :], turn_y(0, "turn_d")[:])
+        nc.scalar.copy(y_t[:, :, 1, :], turn_y(1, "wt_ps")[:])
         turn_w(LAST, "turn_d")
         v_q = sbuf("v_q", [P, D], U32, tag="w_win2")
 
@@ -151,22 +152,12 @@ def tile_attend_glch_pl_x_ts_kernel(tc, xT, wT, y, wt, ts, offs, out_0, out_1, o
                 w_b[v][:].rearrange("p s m j -> p m j s"),
                 w_all[:].rearrange("p (j m s) -> p m j s", j=L, s=L)[:, :, :, PAIR * v : PAIR * (v + 1)],
             )
-        y1_ps = [ps.tile([P, PAIR, P], F32, name="y1_ps%d" % v, tag=("turn_b", "turn_c")[v]) for v in pairs]
-        for e in range(PAIR):
-            for v in pairs:
-                nc.tensor.transpose(y1_ps[v][:, e, :], y_raw[1][:, PAIR * v + e :: L], ident_f[:])
-        for v in pairs:
-            nc.scalar.copy(y_t[0][:, PAIR * v : PAIR * (v + 1), 1, :], y1_ps[v][:])
-        y_ps.append(None)
-        for t in range(PAIR, L):
-            y_ps.append(ps.tile([P, L, P], F32, name="y_ps%d" % t, tag=("turn_b", "wt_ps")[t % PAIR]))
-            turn_y(t)
+        y2_ps = turn_y(2, "turn_c")
         for v in pairs:
             slots = slice(v * PAIR * P, (v + 1) * PAIR * P)
             nc.vector.quantize_mx(
                 w_q[:, slots].bitcast(E4M3), w_s[:, slots], w_b[v][:].rearrange("p s m j -> p (s m j)")
             )
-
         quantise_v(1)
 
         x_b = [sbuf("x_b%d" % u, [P, PAIR, P, L], BF16, tag=("ts_win", "w_b1")[u]) for u in pairs]
@@ -180,31 +171,34 @@ def tile_attend_glch_pl_x_ts_kernel(tc, xT, wT, y, wt, ts, offs, out_0, out_1, o
             nc.vector.quantize_mx(
                 x_q[:, rows].bitcast(E4M3), x_s[:, rows], x_b[u][:].rearrange("p t m j -> p (t m j)")
             )
-        y_t.append(sbuf("y_t1", [P, L, PAIR, P], F32, tag="x_raw"))
-        for t in range(PAIR, L):
-            copy_y(t)
+        y2_t = sbuf("y2_t", [P, L, P], F32, tag="x_raw")
+        nc.scalar.copy(y2_t[:], y2_ps[:])
 
-        mx_banks = ("mx0", "mx1", "mx2", "turn_a")
-        first_banks = [ps.tile([P, PAIR * P], F32, name="score0%d" % s, tag=mx_banks[s]) for s in lanes]
-        second_banks = [
-            ps.tile([P, PAIR, PAIR * P], F32, name="score1%d" % v, tag=("turn_c", "turn_d")[v]) for v in pairs
-        ]
-        score = [[first_banks[s][:] for s in lanes], [second_banks[s // PAIR][:, s % PAIR, :] for s in lanes]]
-        for u in pairs:
-            rows = slice(u * PAIR * P, (u + 1) * PAIR * P)
-            for s in lanes:
-                slots = slice(s * P, (s + 1) * P)
-                nc.tensor.matmul_mx(
-                    score[u][s],
-                    lhsT=w_q[:, slots].bitcast(E4M3),
-                    lhsT_scale=w_s[:, slots],
-                    rhs=x_q[:, rows].bitcast(E4M3),
-                    rhs_scale=x_s[:, rows],
-                    start=True,
-                    stop=True,
-                )
+        def mx(out, lq, ls, rq, rs):
+            nc.tensor.matmul_mx(
+                out, lhsT=lq.bitcast(E4M3), lhsT_scale=ls, rhs=rq.bitcast(E4M3), rhs_scale=rs, start=True, stop=True
+            )
 
-        z = [sbuf("z%d" % u, [P, L, PAIR, P], F32) for u in pairs]
+        mx_banks = ("mx0", "mx1", "turn_d", "turn_a")
+        score01 = [ps.tile([P, PAIR * P], F32, name="score01_%d" % s, tag=mx_banks[s]) for s in lanes]
+        for s in lanes:
+            slots = slice(s * P, (s + 1) * P)
+            mx(score01[s][:], w_q[:, slots], w_s[:, slots], x_q[:, : PAIR * P], x_s[:, : PAIR * P])
+        score3 = ps.tile([P, N], F32, name="score3", tag="wt_ps")
+        mx(score3[:], x_q[:, LAST * P :], x_s[:, LAST * P :], w_q[:], w_s[:])
+        score2 = ps.tile([P, L, P], F32, name="score2", tag="turn_b")
+        for s in lanes:
+            slots = slice(s * P, (s + 1) * P)
+            mx(score2[:, s, :], w_q[:, slots], w_s[:, slots], x_q[:, 2 * P : LAST * P], x_s[:, 2 * P : LAST * P])
+        sum3 = ps.tile([P, L, P], F32, name="sum3", tag="sum3")
+        for s in lanes:
+            nc.tensor.matmul(
+                sum3[:, s, :], y_raw[LAST][:, s::L], ident_f[:], start=s == 0, stop=False, is_transpose=True
+            )
+
+        z01 = sbuf("z01", [P, L, PAIR, P], F32)
+        z2 = sbuf("z2", [P, L, P], F32)
+        a3_neg = sbuf("a3_neg", [P, N], F32)
         th = [sbuf("th%d" % t, [P, P, L], F32) for t in lanes]
         h_b = [sbuf("h_b%d" % t, [P, P * L], BF16) for t in lanes]
         h_q = [sbuf("h_q%d" % t, [P, P], U32) for t in lanes]
@@ -212,22 +206,31 @@ def tile_attend_glch_pl_x_ts_kernel(tc, xT, wT, y, wt, ts, offs, out_0, out_1, o
         g = sbuf("g", [P, L * D], F32)
         out_rows = out_0[0].rearrange("(m t) d -> m t d", t=L)
 
-        def residual(u):
-            for s in lanes:
-                nc.vector.scalar_tensor_tensor(
-                    z[u][:, s].rearrange("p e m -> p (e m)"),
-                    score[u][s],
-                    ts_col[:, s : s + 1],
-                    y_t[u][:, s].rearrange("p e m -> p (e m)"),
-                    MULT,
-                    SUB,
-                )
-            for e in range(PAIR):
-                nc.scalar.activation(
-                    th[PAIR * u + e][:].rearrange("p (c n) s -> p c s n", n=RUN),
-                    z[u][:, :, e, :].rearrange("p s (c n) -> p c s n", n=RUN),
-                    TANH,
-                )
+        def tanh_of(t, z):
+            nc.scalar.activation(
+                th[t][:].rearrange("p (c n) s -> p c s n", n=RUN), z.rearrange("p s (c n) -> p c s n", n=RUN), TANH
+            )
+
+        for s in lanes:
+            nc.vector.scalar_tensor_tensor(
+                z01[:, s].rearrange("p e m -> p (e m)"),
+                score01[s][:],
+                ts_col[:, s : s + 1],
+                y_t[:, s].rearrange("p e m -> p (e m)"),
+                MULT,
+                SUB,
+            )
+        for e in range(PAIR):
+            tanh_of(e, z01[:, :, e, :])
+        nc.vector.tensor_tensor(a3_neg[:], score3[:], ts_neg[:].rearrange("p s m -> p (s m)"), MULT)
+        for s in lanes:
+            nc.tensor.matmul(
+                sum3[:, s, :], a3_neg[:, s * P : (s + 1) * P], ident_f[:], start=False, stop=s == LAST, is_transpose=True
+            )
+        for s in lanes:
+            nc.vector.scalar_tensor_tensor(z2[:, s], score2[:, s, :], ts_col[:, s : s + 1], y2_t[:, s], MULT, SUB)
+        tanh_of(2, z2[:])
+        nc.scalar.activation(th[LAST][:], sum3[:].rearrange("p s m -> p m s"), TANH, scale=-1.0)
 
         def weigh(t, parts, which=None):
             for k in range(parts) if which is None else [which]:
@@ -262,18 +265,6 @@ def tile_attend_glch_pl_x_ts_kernel(tc, xT, wT, y, wt, ts, offs, out_0, out_1, o
                 )
             nc.sync.dma_start(out_rows[:, t, :], g[:, t * D : (t + 1) * D])
 
-        residual(0)
-        residual(1)
-        warm = ps.tile([P, R], F32, name="warm", tag="turn_d")
-        nc.tensor.matmul_mx(
-            warm[:],
-            lhsT=w_q[:, :P].bitcast(E4M3),
-            lhsT_scale=w_s[:, :P],
-            rhs=x_q[:].bitcast(E4M3),
-            rhs_scale=x_s[:],
-            start=True,
-            stop=True,
-        )
         weigh(0, parts=1)
         weigh(1, parts=1)
         back(0, parts=1)

@@ -25,7 +25,7 @@ L = 4
 LAST = L - 1
 PAIR = 2
 RUN = 4
-X_SPLIT = 5 * P // 8
+X_SPLIT = 3 * P // 8
 QUADRANT = 32
 
 
@@ -137,9 +137,13 @@ def tile_attend_glch_pl_x_ts_kernel(tc, xT, wT, y, wt, ts, offs, out_0, out_1, o
         gather(2)
         turn_w(2, "turn_b")
         gather(LAST)
-        nc.scalar.copy(y_t[:, :, 0, :], turn_y(0, "turn_d")[:])
-        nc.scalar.copy(y_t[:, :, 1, :], turn_y(1, "wt_ps")[:])
+        for v in pairs:
+            y0_ps = ps.tile([P, PAIR, P], F32, name="y0_ps%d" % v, tag=("turn_d", "mx0")[v])
+            for e in range(PAIR):
+                nc.tensor.transpose(y0_ps[:, e, :], y_raw[0][:, PAIR * v + e :: L], ident_f[:])
+            nc.scalar.copy(y_t[:, PAIR * v : PAIR * (v + 1), 0, :], y0_ps[:])
         turn_w(LAST, "turn_d")
+        nc.scalar.copy(y_t[:, :, 1, :], turn_y(1, "wt_ps")[:])
         v_q = sbuf("v_q", [P, D], U32, tag="w_win2")
 
         def quantise_v(u):
@@ -164,8 +168,10 @@ def tile_attend_glch_pl_x_ts_kernel(tc, xT, wT, y, wt, ts, offs, out_0, out_1, o
         for u in pairs:
             x_to = x_b[u][:].rearrange("p t m j -> p m j t")
             x_from = x_raw[:].rearrange("p j (m t) -> p m j t", t=L)[:, :, :, PAIR * u : PAIR * (u + 1)]
-            nc.vector.tensor_copy(x_to[:, :X_SPLIT], x_from[:, :X_SPLIT])
-            nc.scalar.copy(x_to[:, X_SPLIT:], x_from[:, X_SPLIT:])
+            split = (P, X_SPLIT)[u]
+            nc.vector.tensor_copy(x_to[:, :split], x_from[:, :split])
+            if split < P:
+                nc.scalar.copy(x_to[:, split:], x_from[:, split:])
         for u in pairs:
             rows = slice(u * PAIR * P, (u + 1) * PAIR * P)
             nc.vector.quantize_mx(
@@ -184,13 +190,19 @@ def tile_attend_glch_pl_x_ts_kernel(tc, xT, wT, y, wt, ts, offs, out_0, out_1, o
         for s in lanes:
             slots = slice(s * P, (s + 1) * P)
             mx(score01[s][:], w_q[:, slots], w_s[:, slots], x_q[:, : PAIR * P], x_s[:, : PAIR * P])
-        score3 = ps.tile([P, N], F32, name="score3", tag="wt_ps")
-        mx(score3[:], x_q[:, LAST * P :], x_s[:, LAST * P :], w_q[:], w_s[:])
-        score2 = ps.tile([P, L, P], F32, name="score2", tag="turn_b")
+        score2 = [ps.tile([P, PAIR, P], F32, name="score2_%d" % v, tag=("turn_b", "spare")[v]) for v in pairs]
         for s in lanes:
             slots = slice(s * P, (s + 1) * P)
-            mx(score2[:, s, :], w_q[:, slots], w_s[:, slots], x_q[:, 2 * P : LAST * P], x_s[:, 2 * P : LAST * P])
-        sum3 = ps.tile([P, L, P], F32, name="sum3", tag="sum3")
+            mx(
+                score2[s // PAIR][:, s % PAIR, :],
+                w_q[:, slots],
+                w_s[:, slots],
+                x_q[:, 2 * P : LAST * P],
+                x_s[:, 2 * P : LAST * P],
+            )
+        score3 = ps.tile([P, N], F32, name="score3", tag="wt_ps")
+        mx(score3[:], x_q[:, LAST * P :], x_s[:, LAST * P :], w_q[:], w_s[:])
+        sum3 = ps.tile([P, L, P], F32, name="sum3", tag="turn_c")
         for s in lanes:
             nc.tensor.matmul(
                 sum3[:, s, :], y_raw[LAST][:, s::L], ident_f[:], start=s == 0, stop=False, is_transpose=True
@@ -222,14 +234,16 @@ def tile_attend_glch_pl_x_ts_kernel(tc, xT, wT, y, wt, ts, offs, out_0, out_1, o
             )
         for e in range(PAIR):
             tanh_of(e, z01[:, :, e, :])
+        for s in lanes:
+            nc.vector.scalar_tensor_tensor(
+                z2[:, s], score2[s // PAIR][:, s % PAIR, :], ts_col[:, s : s + 1], y2_t[:, s], MULT, SUB
+            )
+        tanh_of(2, z2[:])
         nc.vector.tensor_tensor(a3_neg[:], score3[:], ts_neg[:].rearrange("p s m -> p (s m)"), MULT)
         for s in lanes:
             nc.tensor.matmul(
                 sum3[:, s, :], a3_neg[:, s * P : (s + 1) * P], ident_f[:], start=False, stop=s == LAST, is_transpose=True
             )
-        for s in lanes:
-            nc.vector.scalar_tensor_tensor(z2[:, s], score2[:, s, :], ts_col[:, s : s + 1], y2_t[:, s], MULT, SUB)
-        tanh_of(2, z2[:])
         nc.scalar.activation(th[LAST][:], sum3[:].rearrange("p s m -> p m s"), TANH, scale=-1.0)
 
         def weigh(t, parts, which=None):

@@ -54,13 +54,15 @@ def tile_attend_glch_pl_x_ts_kernel(tc, xT, wT, y, wt, ts, offs, out_0, out_1, o
         nc.sync.dma_start(wt_col[:], wt[0].rearrange("(m t) o -> m (t o)", t=L))
         nc.sync.dma_start(ts_win[P - 1 : P, :], ts[0:1, :])
         y_rows = y[0].rearrange("(m t) i -> m t i", t=L)
-        y_raw = [sbuf("y_raw%d" % t, [P, N], F32) for t in lanes]
+        y_ends = [sbuf("y_end%d" % e, [P, N], F32) for e in range(PAIR)]
+        y_mid = sbuf("y_mid", [P, PAIR, N], F32)
+        y_raw = [y_ends[0][:], y_mid[:, 0], y_mid[:, 1], y_ends[1][:]]
         for j in range(1, L):
             nc.sync.dma_start(w_win[j][:], w_rows[:, j, :])
-        for t in range(0, LAST):
-            nc.sync.dma_start(y_raw[t][:], y_rows[:, t, :])
+        nc.sync.dma_start(y_raw[0], y_rows[:, 0, :])
+        nc.sync.dma_start(y_mid[:], y_rows[:, 1:LAST, :])
         nc.sync.dma_start(x_raw[:], xT[0].rearrange("(p j) r -> p j r", j=L))
-        nc.sync.dma_start(y_raw[LAST][:], y_rows[:, LAST, :])
+        nc.sync.dma_start(y_raw[LAST], y_rows[:, LAST, :])
 
         ident_f = sbuf("ident_f", [P, P], F32)
         make_identity(nc, ident_f[:])
@@ -190,7 +192,9 @@ def tile_attend_glch_pl_x_ts_kernel(tc, xT, wT, y, wt, ts, offs, out_0, out_1, o
         for s in lanes:
             slots = slice(s * P, (s + 1) * P)
             mx(score01[s][:], w_q[:, slots], w_s[:, slots], x_q[:, : PAIR * P], x_s[:, : PAIR * P])
-        score2 = [ps.tile([P, PAIR, P], F32, name="score2_%d" % v, tag=("turn_b", "spare")[v]) for v in pairs]
+        score3 = ps.tile([P, N], F32, name="score3", tag="wt_ps")
+        mx(score3[:], x_q[:, LAST * P :], x_s[:, LAST * P :], w_q[:], w_s[:])
+        score2 = [ps.tile([P, PAIR, P], F32, name="score2_%d" % v, tag=("turn_b", "mx0")[v]) for v in pairs]
         for s in lanes:
             slots = slice(s * P, (s + 1) * P)
             mx(
@@ -200,18 +204,25 @@ def tile_attend_glch_pl_x_ts_kernel(tc, xT, wT, y, wt, ts, offs, out_0, out_1, o
                 x_q[:, 2 * P : LAST * P],
                 x_s[:, 2 * P : LAST * P],
             )
-        score3 = ps.tile([P, N], F32, name="score3", tag="wt_ps")
-        mx(score3[:], x_q[:, LAST * P :], x_s[:, LAST * P :], w_q[:], w_s[:])
-        sum3 = ps.tile([P, L, P], F32, name="sum3", tag="turn_c")
-        for s in lanes:
+        sum3 = [ps.tile([P, PAIR, P], F32, name="sum3_%d" % v, tag=("spare", "turn_c")[v]) for v in pairs]
+
+        def add_turn(s, in_, first):
             nc.tensor.matmul(
-                sum3[:, s, :], y_raw[LAST][:, s::L], ident_f[:], start=s == 0, stop=False, is_transpose=True
+                sum3[s // PAIR][:, s % PAIR, :],
+                in_,
+                ident_f[:],
+                start=first and s % PAIR == 0,
+                stop=not first and s % PAIR == 1,
+                is_transpose=True,
             )
+
+        for s in lanes:
+            add_turn(s, y_raw[LAST][:, s::L], first=True)
 
         z01 = sbuf("z01", [P, L, PAIR, P], F32)
         z2 = sbuf("z2", [P, L, P], F32)
         a3_neg = sbuf("a3_neg", [P, N], F32)
-        th = [sbuf("th%d" % t, [P, P, L], F32) for t in lanes]
+        th = [sbuf("th%d" % t, [P, P, L], F32) for t in range(LAST)]
         h_b = [sbuf("h_b%d" % t, [P, P * L], BF16) for t in lanes]
         h_q = [sbuf("h_q%d" % t, [P, P], U32) for t in lanes]
         h_s = [sbuf("h_s%d" % t, [P, P], U8) for t in lanes]
@@ -234,23 +245,30 @@ def tile_attend_glch_pl_x_ts_kernel(tc, xT, wT, y, wt, ts, offs, out_0, out_1, o
             )
         for e in range(PAIR):
             tanh_of(e, z01[:, :, e, :])
+        nc.vector.tensor_tensor(a3_neg[:], score3[:], ts_neg[:].rearrange("p s m -> p (s m)"), MULT)
+        for s in lanes:
+            add_turn(s, a3_neg[:, s * P : (s + 1) * P], first=False)
         for s in lanes:
             nc.vector.scalar_tensor_tensor(
                 z2[:, s], score2[s // PAIR][:, s % PAIR, :], ts_col[:, s : s + 1], y2_t[:, s], MULT, SUB
             )
         tanh_of(2, z2[:])
-        nc.vector.tensor_tensor(a3_neg[:], score3[:], ts_neg[:].rearrange("p s m -> p (s m)"), MULT)
-        for s in lanes:
-            nc.tensor.matmul(
-                sum3[:, s, :], a3_neg[:, s * P : (s + 1) * P], ident_f[:], start=False, stop=s == LAST, is_transpose=True
-            )
-        nc.scalar.activation(th[LAST][:], sum3[:].rearrange("p s m -> p m s"), TANH, scale=-1.0)
+        th3 = sbuf("th3_pairs", [P, PAIR, P, PAIR], F32)
+        for v in pairs:
+            nc.scalar.activation(th3[:, v], sum3[v][:].rearrange("p e m -> p m e"), TANH, scale=-1.0)
 
         def weigh(t, parts, which=None):
             for k in range(parts) if which is None else [which]:
                 ms = slice(k * P // parts, (k + 1) * P // parts)
+                if t < LAST:
+                    th_t = th[t][:].rearrange("p m (v e) -> p m v e", v=PAIR)
+                else:
+                    th_t = th3[:].rearrange("p v m e -> p m v e")
                 nc.vector.tensor_tensor(
-                    h_b[t][:].rearrange("p (m s) -> p m s", s=L)[:, ms], th[t][:, ms], factor[t][:, ms], MULT
+                    h_b[t][:].rearrange("p (m v e) -> p m v e", v=PAIR, e=PAIR)[:, ms],
+                    th_t[:, ms],
+                    factor[t].rearrange("p m (v e) -> p m v e", v=PAIR)[:, ms],
+                    MULT,
                 )
 
         def back(t, parts):

@@ -97,8 +97,8 @@ def tile_attend_glch_pl_x_ts_kernel(tc, xT, wT, y, wt, ts, offs, out_0, out_1, o
             for v in pairs:
                 nc.tensor.transpose(w_ps[:, v, :], words[:, v::PAIR], ident_f[:])
             nc.scalar.copy(
-                v_b[j // PAIR][:, j % PAIR * N : (j % PAIR + 1) * N].bitcast(F32).rearrange("m (p v) -> m p v", v=PAIR),
-                w_ps[:].rearrange("m v p -> m p v"),
+                v_b[j // PAIR][:].bitcast(F32).rearrange("m (h e p v) -> m h e p v", h=PAIR, e=PAIR, v=PAIR)[:, :, j % PAIR],
+                w_ps[:].rearrange("m v (h p) -> m h p v", h=PAIR),
             )
 
         def turn_y(t, bank):
@@ -271,6 +271,19 @@ def tile_attend_glch_pl_x_ts_kernel(tc, xT, wT, y, wt, ts, offs, out_0, out_1, o
                     MULT,
                 )
 
+        half_banks = ("turn_b", "spare")
+
+        def product(out, t, cols):
+            nc.tensor.matmul_mx(
+                out,
+                lhsT=h_q[t][:].bitcast(E5M2),
+                lhsT_scale=h_s[t][:],
+                rhs=v_q[:, cols].bitcast(E4M3),
+                rhs_scale=v_s[:, cols],
+                start=True,
+                stop=True,
+            )
+
         def back(t, parts):
             for k in range(parts):
                 ms = slice(k * P // parts, (k + 1) * P // parts)
@@ -279,27 +292,23 @@ def tile_attend_glch_pl_x_ts_kernel(tc, xT, wT, y, wt, ts, offs, out_0, out_1, o
                     h_s[t][:, ms],
                     h_b[t][:, k * P * L // parts : (k + 1) * P * L // parts],
                 )
-            acc = ps.tile([P, L, P], F32, name="acc%d" % t, tag=mx_banks[t])
-            nc.tensor.matmul_mx(
-                acc[:].rearrange("m j p -> m (j p)"),
-                lhsT=h_q[t][:].bitcast(E5M2),
-                lhsT_scale=h_s[t][:],
-                rhs=v_q[:].bitcast(E4M3),
-                rhs_scale=v_s[:],
-                start=True,
-                stop=True,
-            )
-            width = D // parts
-            for k in range(parts):
-                nc.scalar.copy(
-                    g[:, t * D + k * width : t * D + (k + 1) * width].rearrange("m (p j) -> m p j", j=L),
-                    acc[:, :, k * width // L : (k + 1) * width // L].rearrange("m j p -> m p j"),
-                )
+            g_t = g[:, t * D : (t + 1) * D].rearrange("m (h p u e) -> m h p u e", h=PAIR, u=PAIR, e=PAIR)
+            if t < PAIR:
+                acc = ps.tile([P, D], F32, name="acc%d" % t, tag=mx_banks[t])
+                product(acc[:], t, slice(0, D))
+                nc.scalar.copy(g_t, acc[:].rearrange("m (u h e p) -> m h p u e", u=PAIR, h=PAIR, e=PAIR))
+            else:
+                for h in range(PAIR):
+                    acc = ps.tile([P, PAIR, P], F32, name="acc%d_%d" % (t, h), tag=(mx_banks[t], half_banks[t % PAIR])[h])
+                    for u in pairs:
+                        product(acc[:, u, :], t, slice((PAIR * u + h) * P, (PAIR * u + h + 1) * P))
+                    nc.scalar.copy(g_t[:, h], acc[:].rearrange("m u (e p) -> m p u e", e=PAIR))
             nc.sync.dma_start(out_rows[:, t, :], g[:, t * D : (t + 1) * D])
 
         weigh(0, parts=1)
-        weigh(1, parts=1)
+        weigh(1, parts=2, which=0)
         back(0, parts=1)
+        weigh(1, parts=2, which=1)
         back(1, parts=1)
         weigh(2, parts=1)
         weigh(LAST, parts=2, which=0)

@@ -306,9 +306,8 @@ def tile_attend_glch_pl_x_ts_kernel(tc, xT, wT, y, wt, ts, offs, out_0, out_1, o
             nc.sync.dma_start(out_rows[:, t, :], g[:, t * D : (t + 1) * D])
 
         weigh(0, parts=1)
-        weigh(1, parts=2, which=0)
+        weigh(1, parts=1)
         back(0, parts=1)
-        weigh(1, parts=2, which=1)
         back(1, parts=1)
         weigh(2, parts=1)
         weigh(LAST, parts=2, which=0)

from contextlib import ExitStack

import concourse.mybir as mybir
from concourse.masks import make_identity

N, T, D, R = 512, 2048, 512, 512
FLOPS = 2 * 2 * N * D * R
BYTES = 4 * (D * R + D * T + R * N + R + T + R * D) + 2 * 128 * (N // 16) + R * D + (R // 32) * D

F32 = mybir.dt.float32
BF16 = mybir.dt.bfloat16
I32 = mybir.dt.int32
U32 = mybir.dt.uint32
U16 = mybir.dt.uint16
U8 = mybir.dt.uint8
E4M3 = mybir.dt.float8_e4m3fn_x4
E5M2 = mybir.dt.float8_e5m2_x4
MULT = mybir.AluOpType.mult
SUB = mybir.AluOpType.subtract
COPY = mybir.ActivationFunctionType.Copy
TANH = mybir.ActivationFunctionType.Tanh

P = 128
L = 4
LAST = L - 1
PAIR = 2
RUN = 4
X_SPLIT = 3 * P // 8
QUADRANT = 32


def tile_attend_glch_pl_x_ts_kernel(tc, xT, wT, y, wt, ts, offs, out_0, out_1, out_2):
    nc = tc.nc
    lanes = range(L)
    pairs = range(L // PAIR)
    with ExitStack() as ctx:
        sb = ctx.enter_context(tc.tile_pool(name="sb", bufs=1))
        ps = ctx.enter_context(tc.psum_pool(name="ps", bufs=1))

        def sbuf(name, shape, dtype, tag=None):
            return sb.tile(shape, dtype, name=name, tag=tag or name, align_bytes=64)

        offsets = sb.tile([P, N // 16], U16, name="offsets")

        ts_win = sbuf("ts_win", [P, T], F32)
        nc.vector.memset(ts_win[: P - 1, :], 0.0)

        x_raw = sbuf("x_raw", [P, L, R], F32)
        w_rows = wT.rearrange("(p j) c -> p j c", j=L)
        w_win = [sbuf("w_win%d" % j, [P, T], F32) for j in lanes]
        nc.sync.dma_start(w_win[0][:], w_rows[:, 0, :])
        nc.sync.dma_start(offsets[:], offs)
        wt_col = sbuf("wt_col", [P, L], F32)
        nc.sync.dma_start(wt_col[:], wt[0].rearrange("(m t) o -> m (t o)", t=L))
        nc.sync.dma_start(ts_win[P - 1 : P, :], ts[0:1, :])
        y_rows = y[0].rearrange("(m t) i -> m t i", t=L)
        y_ends = [sbuf("y_end%d" % e, [P, N], F32) for e in range(PAIR)]
        y_mid = sbuf("y_mid", [P, PAIR, N], F32)
        y_raw = [y_ends[0][:], y_mid[:, 0], y_mid[:, 1], y_ends[1][:]]
        for j in range(1, L):
            nc.sync.dma_start(w_win[j][:], w_rows[:, j, :])
        nc.sync.dma_start(y_raw[0], y_rows[:, 0, :])
        nc.sync.dma_start(y_mid[:], y_rows[:, 1:LAST, :])
        nc.sync.dma_start(x_raw[:], xT[0].rearrange("(p j) r -> p j r", j=L))
        nc.sync.dma_start(y_raw[LAST], y_rows[:, LAST, :])

        ident_f = sbuf("ident_f", [P, P], F32)
        make_identity(nc, ident_f[:])

        wt_ps = ps.tile([P, L, P], F32, name="wt_ps", tag="wt_ps")
        for t in lanes:
            nc.tensor.transpose(wt_ps[:, t, :], wt_col[:, t : t + 1].to_broadcast([P, P]), ident_f[:])

        ts_g = sbuf("ts_g", [P, N], F32)
        nc.vector.tensor_copy(ts_g[:], ts_win[:].indirect(offsets[:]))
        x_q = sbuf("x_q", [P, R], U32)
        x_s = sbuf("x_s", [P, R], U8)

        ts_ps = ps.tile([P, L, P], F32, name="ts_ps", tag="turn_a")
        for s in lanes:
            nc.tensor.transpose(ts_ps[:, s, :], ts_g[:, s::L], ident_f[:])
        ts_col = sbuf("ts_col", [P, L], F32)
        nc.scalar.copy(ts_col[:], ts_ps[:, :, P - 1])

        w_b = [sbuf("w_b%d" % v, [P, PAIR, P, L], BF16) for v in pairs]
        w_all = sbuf("w_all", [P, L * N], BF16, tag="ts_win")
        w_flat = [w_all[:, j * N : (j + 1) * N] for j in lanes]
        v_b = [sbuf("v_b%d" % u, [P, PAIR * N], BF16) for u in pairs]
        y_t = sbuf("y_t", [P, L, PAIR, P], F32)

        def gather(j):
            nc.vector.tensor_copy(w_flat[j], w_win[j][:].indirect(offsets[:]))

        def turn_w(j, bank):
            w_ps = ps.tile([P, PAIR, P], F32, name="w_ps%d" % j, tag=bank)
            words = w_flat[j].bitcast(F32)
            for v in pairs:
                nc.tensor.transpose(w_ps[:, v, :], words[:, v::PAIR], ident_f[:])
            nc.scalar.copy(
                v_b[j // PAIR][:].bitcast(F32).rearrange("m (h e p v) -> m h e p v", h=PAIR, e=PAIR, v=PAIR)[:, :, j % PAIR],
                w_ps[:].rearrange("m v (h p) -> m h p v", h=PAIR),
            )

        def turn_y(t, bank):
            y_ps = ps.tile([P, L, P], F32, name="y_ps%d" % t, tag=bank)
            for s in lanes:
                nc.tensor.transpose(y_ps[:, s, :], y_raw[t][:, s::L], ident_f[:])
            return y_ps

        v_s = sbuf("v_s", [P, D], U8)
        w_q = sbuf("w_q", [P, N], U32)
        w_s = sbuf("w_s", [P, N], U8)

        gather(0)
        turn_w(0, "turn_a")
        factor_flat = sbuf("factor_flat", [P, L, LAST, P], F32)
        for s in lanes:
            nc.scalar.activation(factor_flat[:, s], wt_ps[:, 1:L], COPY, scale=ts_col[:, s : s + 1])
        ts_row_ps = ps.tile([P, L, P], F32, name="ts_row_ps", tag="turn_b")
        for s in lanes:
            nc.tensor.transpose(ts_row_ps[:, s, :], ts_col[:, s : s + 1].to_broadcast([P, P]), ident_f[:])
        ts_neg = sbuf("ts_neg", [P, L, P], F32)
        nc.scalar.activation(ts_neg[:], ts_row_ps[:], COPY, scale=-1.0)
        gather(1)
        turn_w(1, "turn_a")
        factor_all = sbuf("factor_all", [P, L, P, L], F32, tag="w_win1")
        factor = [factor_all[:, t] for t in lanes]
        nc.vector.tensor_tensor(
            factor[0],
            wt_ps[:, 0, :].unsqueeze(2).broadcast_to([P, P, L]),
            ts_col[:].unsqueeze(1).broadcast_to([P, P, L]),
            MULT,
        )
        for t in range(1, L):
            nc.scalar.copy(
                factor[t].rearrange("p (c n) s -> p c s n", n=RUN),
                factor_flat[:, :, t - 1, :].rearrange("p s (c n) -> p c s n", n=RUN),
            )
        gather(2)
        turn_w(2, "turn_b")
        gather(LAST)
        for v in pairs:
            y0_ps = ps.tile([P, PAIR, P], F32, name="y0_ps%d" % v, tag=("turn_d", "mx0")[v])
            for e in range(PAIR):
                nc.tensor.transpose(y0_ps[:, e, :], y_raw[0][:, PAIR * v + e :: L], ident_f[:])
            nc.scalar.copy(y_t[:, PAIR * v : PAIR * (v + 1), 0, :], y0_ps[:])
        turn_w(LAST, "turn_d")
        nc.scalar.copy(y_t[:, :, 1, :], turn_y(1, "wt_ps")[:])
        v_q = sbuf("v_q", [P, D], U32, tag="w_win2")

        def quantise_v(u):
            cols = slice(u * PAIR * P, (u + 1) * PAIR * P)
            nc.vector.quantize_mx(v_q[:, cols].bitcast(E4M3), v_s[:, cols], v_b[u][:])

        quantise_v(0)
        for v in pairs:
            nc.vector.tensor_copy(
                w_b[v][:].rearrange("p s m j -> p m j s"),
                w_all[:].rearrange("p (j m s) -> p m j s", j=L, s=L)[:, :, :, PAIR * v : PAIR * (v + 1)],
            )
        y2_ps = turn_y(2, "turn_c")
        for v in pairs:
            slots = slice(v * PAIR * P, (v + 1) * PAIR * P)
            nc.vector.quantize_mx(
                w_q[:, slots].bitcast(E4M3), w_s[:, slots], w_b[v][:].rearrange("p s m j -> p (s m j)")
            )
        quantise_v(1)

        x_b = [sbuf("x_b%d" % u, [P, PAIR, P, L], BF16, tag=("ts_win", "w_b1")[u]) for u in pairs]
        for u in pairs:
            x_to = x_b[u][:].rearrange("p t m j -> p m j t")
            x_from = x_raw[:].rearrange("p j (m t) -> p m j t", t=L)[:, :, :, PAIR * u : PAIR * (u + 1)]
            split = (P, X_SPLIT)[u]
            nc.vector.tensor_copy(x_to[:, :split], x_from[:, :split])
            if split < P:
                nc.scalar.copy(x_to[:, split:], x_from[:, split:])
        for u in pairs:
            rows = slice(u * PAIR * P, (u + 1) * PAIR * P)
            nc.vector.quantize_mx(
                x_q[:, rows].bitcast(E4M3), x_s[:, rows], x_b[u][:].rearrange("p t m j -> p (t m j)")
            )
        y2_t = sbuf("y2_t", [P, L, P], F32, tag="x_raw")
        nc.scalar.copy(y2_t[:], y2_ps[:])

        def mx(out, lq, ls, rq, rs):
            nc.tensor.matmul_mx(
                out, lhsT=lq.bitcast(E4M3), lhsT_scale=ls, rhs=rq.bitcast(E4M3), rhs_scale=rs, start=True, stop=True
            )

        mx_banks = ("mx0", "mx1", "turn_d", "turn_a")
        score01 = [ps.tile([P, PAIR * P], F32, name="score01_%d" % s, tag=mx_banks[s]) for s in lanes]
        for s in lanes:
            slots = slice(s * P, (s + 1) * P)
            mx(score01[s][:], w_q[:, slots], w_s[:, slots], x_q[:, : PAIR * P], x_s[:, : PAIR * P])
        score3 = ps.tile([P, N], F32, name="score3", tag="wt_ps")
        mx(score3[:], x_q[:, LAST * P :], x_s[:, LAST * P :], w_q[:], w_s[:])
        score2 = [ps.tile([P, PAIR, P], F32, name="score2_%d" % v, tag=("turn_b", "mx0")[v]) for v in pairs]
        for s in lanes:
            slots = slice(s * P, (s + 1) * P)
            mx(
                score2[s // PAIR][:, s % PAIR, :],
                w_q[:, slots],
                w_s[:, slots],
                x_q[:, 2 * P : LAST * P],
                x_s[:, 2 * P : LAST * P],
            )
        sum3 = [ps.tile([P, PAIR, P], F32, name="sum3_%d" % v, tag=("spare", "turn_c")[v]) for v in pairs]

        def add_turn(s, in_, first):
            nc.tensor.matmul(
                sum3[s // PAIR][:, s % PAIR, :],
                in_,
                ident_f[:],
                start=first and s % PAIR == 0,
                stop=not first and s % PAIR == 1,
                is_transpose=True,
            )

        for s in lanes:
            add_turn(s, y_raw[LAST][:, s::L], first=True)

        z01 = sbuf("z01", [P, L, PAIR, P], F32)
        z2 = sbuf("z2", [P, L, P], F32)
        a3_neg = sbuf("a3_neg", [P, N], F32)
        th = [sbuf("th%d" % t, [P, P, L], F32) for t in range(LAST)]
        h_b = [sbuf("h_b%d" % t, [P, P * L], BF16) for t in lanes]
        h_q = [sbuf("h_q%d" % t, [P, P], U32) for t in lanes]
        h_s = [sbuf("h_s%d" % t, [P, P], U8) for t in lanes]
        g = sbuf("g", [P, L * D], F32)
        out_rows = out_0[0].rearrange("(m t) d -> m t d", t=L)

        def tanh_of(t, z):
            nc.scalar.activation(
                th[t][:].rearrange("p (c n) s -> p c s n", n=RUN), z.rearrange("p s (c n) -> p c s n", n=RUN), TANH
            )

        for s in lanes:
            nc.vector.scalar_tensor_tensor(
                z01[:, s].rearrange("p e m -> p (e m)"),
                score01[s][:],
                ts_col[:, s : s + 1],
                y_t[:, s].rearrange("p e m -> p (e m)"),
                MULT,
                SUB,
            )
        for e in range(PAIR):
            tanh_of(e, z01[:, :, e, :])
        nc.vector.tensor_tensor(a3_neg[:], score3[:], ts_neg[:].rearrange("p s m -> p (s m)"), MULT)
        for s in lanes:
            add_turn(s, a3_neg[:, s * P : (s + 1) * P], first=False)
        for s in lanes:
            nc.vector.scalar_tensor_tensor(
                z2[:, s], score2[s // PAIR][:, s % PAIR, :], ts_col[:, s : s + 1], y2_t[:, s], MULT, SUB
            )
        tanh_of(2, z2[:])
        th3 = sbuf("th3_pairs", [P, PAIR, P, PAIR], F32)
        for v in pairs:
            nc.scalar.activation(th3[:, v], sum3[v][:].rearrange("p e m -> p m e"), TANH, scale=-1.0)

        def weigh(t, parts, which=None):
            for k in range(parts) if which is None else [which]:
                ms = slice(k * P // parts, (k + 1) * P // parts)
                if t < LAST:
                    th_t = th[t][:].rearrange("p m (v e) -> p m v e", v=PAIR)
                else:
                    th_t = th3[:].rearrange("p v m e -> p m v e")
                nc.vector.tensor_tensor(
                    h_b[t][:].rearrange("p (m v e) -> p m v e", v=PAIR, e=PAIR)[:, ms],
                    th_t[:, ms],
                    factor[t].rearrange("p m (v e) -> p m v e", v=PAIR)[:, ms],
                    MULT,
                )

        half_banks = ("turn_b", "spare")

        def product(out, t, cols):
            nc.tensor.matmul_mx(
                out,
                lhsT=h_q[t][:].bitcast(E5M2),
                lhsT_scale=h_s[t][:],
                rhs=v_q[:, cols].bitcast(E4M3),
                rhs_scale=v_s[:, cols],
                start=True,
                stop=True,
            )

        def back(t, parts):
            for k in range(parts):
                ms = slice(k * P // parts, (k + 1) * P // parts)
                nc.vector.quantize_mx(
                    h_q[t][:, ms].bitcast(E5M2),
                    h_s[t][:, ms],
                    h_b[t][:, k * P * L // parts : (k + 1) * P * L // parts],
                )
            g_t = g[:, t * D : (t + 1) * D].rearrange("m (h p u e) -> m h p u e", h=PAIR, u=PAIR, e=PAIR)
            if t < PAIR:
                acc = ps.tile([P, D], F32, name="acc%d" % t, tag=mx_banks[t])
                product(acc[:], t, slice(0, D))
                nc.scalar.copy(g_t, acc[:].rearrange("m (u h e p) -> m h p u e", u=PAIR, h=PAIR, e=PAIR))
            else:
                for h in range(PAIR):
                    acc = ps.tile([P, PAIR, P], F32, name="acc%d_%d" % (t, h), tag=(mx_banks[t], half_banks[t % PAIR])[h])
                    for u in pairs:
                        product(acc[:, u, :], t, slice((PAIR * u + h) * P, (PAIR * u + h + 1) * P))
                    nc.scalar.copy(g_t[:, h], acc[:].rearrange("m u (e p) -> m p u e", e=PAIR))
            nc.sync.dma_start(out_rows[:, t, :], g[:, t * D : (t + 1) * D])

        weigh(0, parts=1)
        weigh(1, parts=1)
        back(0, parts=1)
        back(1, parts=1)
        weigh(2, parts=1)
        weigh(LAST, parts=2, which=0)
        back(2, parts=1)
        weigh(LAST, parts=2, which=1)
        back(LAST, parts=2)

        g_b = sbuf("g_b", [P, D, L], BF16)
        g_q = sbuf("g_q", [P, D], U32)
        g_s = sbuf("g_s", [P, D], U8)
        g_from = g[:].rearrange("p (t c n) -> p c t n", t=L, n=RUN)
        g_to = g_b[:].rearrange("p (c n) t -> p c t n", n=RUN)
        nc.vector.tensor_copy(g_to[:, :, 0:PAIR], g_from[:, :, 0:PAIR])
        half = D // 2
        words_out = out_1[0].rearrange("p d l -> p (d l)").bitcast(I32)
        for k in range(2):
            runs = slice(k * half // RUN, (k + 1) * half // RUN)
            nc.vector.tensor_copy(g_to[:, runs, PAIR:L], g_from[:, runs, PAIR:L])
        for k in range(2):
            cols = slice(k * half, (k + 1) * half)
            nc.vector.quantize_mx(
                g_q[:, cols].bitcast(E4M3), g_s[:, cols], g_b[:, cols, :].rearrange("p d t -> p (d t)")
            )
            nc.sync.dma_start(words_out[:, cols], g_q[:, cols].bitcast(I32))
        scale_rows = out_2[0].bitcast(I32)
        for q in range(P // QUADRANT):
            queue = nc.scalar if q % 2 == 0 else nc.sync
            queue.dma_start(scale_rows[L * q : L * (q + 1), :], g_s[QUADRANT * q : QUADRANT * q + L, :].bitcast(I32))
